import numpy as np
import ml_dtypes


def mxq(x, axis, fmt="e4m3"):
    dtype, down = {"e4m3": (ml_dtypes.float8_e4m3fn, 7), "e5m2": (ml_dtypes.float8_e5m2, 14)}[fmt]
    v = np.moveaxis(np.asarray(x, np.float32).astype(ml_dtypes.bfloat16).astype(np.float64), axis, -1)
    blocks = v.reshape(v.shape[:-1] + (-1, 32))
    amax = np.abs(blocks).max(-1, keepdims=True)
    byte = np.maximum(np.where(amax > 0, np.frexp(amax)[1] - 1 + 127, 0) - down, 1)
    scale = np.exp2(byte - 127.0)
    codes = (blocks / scale).astype(np.float32).astype(dtype).astype(np.float64)
    return np.moveaxis((codes * scale).reshape(v.shape), -1, axis)


WIDE = False


def mx_kscale(k):
    if not WIDE:
        return np.ones(k)
    levels = np.array([10, -10, 5, -5, 0])
    if k % 512:
        return np.exp2(np.random.permutation(np.resize(levels, k // 32))).repeat(32)
    a = np.empty((k // 512, 16))
    for p in range(k // 512):
        a[p, :8] = np.random.permutation(np.resize(levels, 8))
        for g in range(8):
            far = levels[np.abs(levels - a[p, g]) >= 10]
            a[p, g + 8] = far[np.random.randint(len(far))]
    return np.exp2(a.ravel()).repeat(32)


def f64(x):
    return np.asarray(x).astype(np.float64)


def striped(idx):
    return np.tile(idx.reshape(-1, 16).T, (8, 1)).astype(np.uint16)


def unstriped(offs):
    return offs[:16].T.reshape(-1).astype(np.int64)


def pack_weight(w):
    k, n = w.shape
    w = f64(np.asarray(w, np.float32).astype(ml_dtypes.bfloat16)).reshape(k // 32, 32, n)
    amax = np.abs(w).max(1)
    byte = np.clip(np.where(amax > 0, np.frexp(amax)[1] - 1 + 127 - 7, 1), 1, 254)
    scaled = (w * np.exp2(127.0 - byte)[:, None, :]).reshape(k, n).astype(np.float32)
    words = np.ascontiguousarray(scaled.reshape(k // 512, 128, 4, n).transpose(0, 1, 3, 2)).astype(ml_dtypes.float8_e4m3fn).view(np.uint8)
    return words, np.ascontiguousarray(byte.astype(np.uint8).reshape(k // 512, 16, n))


def unpack_weight(words, scales):
    g, p, n, _ = words.shape
    vals = np.ascontiguousarray(words).view(ml_dtypes.float8_e4m3fn).astype(np.float64) * np.repeat(np.exp2(scales.astype(np.float64) - 127.0), 8, axis=1)[..., None]
    return vals.transpose(0, 1, 3, 2).reshape(g * 512, n)


K, T, E, C, N = 1024, 512, 8, 128, 128
M = 512


def by_expert(wq, xq):
    return np.concatenate([wq[e].T @ xq[:, e * C:(e + 1) * C] for e in range(E)], axis=1)


def setup_inputs():
    n = np.random.standard_normal
    s = mx_kscale(K)[:, None]
    first = np.random.permutation(np.repeat(np.arange(E), T // E))
    second = (first + 1 + np.random.permutation(np.repeat(np.arange(E - 1), -(-T // (E - 1)))[:T])) % E
    while np.bincount(second, minlength=E).max() != T // E:
        load = np.bincount(second, minlength=E); hi, lo = int(load.argmax()), int(load.argmin())
        t = np.flatnonzero((second == hi) & (first != lo))[0]; second[t] = lo
    slot_token = np.empty(E * C, np.int64); pos = np.empty((2, T), np.int64); fill = np.zeros(E, np.int64)
    place = np.stack([np.random.permutation(C) for _ in range(E)])
    for r, deal in enumerate((first, second)):
        for t in np.random.permutation(T):
            e = deal[t]; j = e * C + place[e, fill[e]]; fill[e] += 1; slot_token[j] = t; pos[r, t] = j
    g = np.random.uniform(0.2, 0.8, T)
    packed = [pack_weight(m) for m in n((E, K, N)) / np.sqrt(K) / s[None]]
    r = mx_kscale(M)[:, None]
    return {
        "uT": (n((M, T)) * r).astype(np.float32),
        "wu": (n((M, K)) / np.sqrt(M) / r * s.T).astype(np.float32),
        "w_words": np.stack([m[0] for m in packed]),
        "w_scales": np.stack([m[1] for m in packed]),
        "b": (0.3 * n((N, E))).astype(np.float32),
        "gate": np.stack([np.tile(g, (N, 1)), np.tile(1.0 - g, (N, 1))]).astype(np.float32),
        "offs": striped(slot_token),
        "pos1": striped(pos[0]),
        "pos2": striped(pos[1]),
    }


def reference(uT, wu, w_words, w_scales, b, gate, offs, pos1, pos2):
    idx = unstriped(offs)
    w = np.stack([unpack_weight(w_words[e], w_scales[e]) for e in range(E)])
    x = mxq(f64(wu), 0, "e4m3").T @ mxq(f64(uT), 0, "e4m3")
    xq = mxq(x[:, idx], 0, "e4m3")
    y = by_expert(w, xq)
    y = y + np.repeat(f64(b), C, axis=1)
    return f64(gate[0]) * y[:, unstriped(pos1)] + f64(gate[1]) * y[:, unstriped(pos2)]

@@ -1,0 +1,234 @@
+from contextlib import ExitStack
+
+import concourse.mybir as mybir
+
+F32 = mybir.dt.float32
+BF16 = mybir.dt.bfloat16
+I32 = mybir.dt.int32
+U32 = mybir.dt.uint32
+U16 = mybir.dt.uint16
+U8 = mybir.dt.uint8
+FP8X4 = mybir.dt.float8_e4m3fn_x4
+MULT = mybir.AluOpType.mult
+ADD = mybir.AluOpType.add
+IDENT = mybir.ActivationFunctionType.Identity
+
+K, T, E, C, N, M = 1024, 512, 8, 128, 128, 512
+P = 128
+S = E * C
+PASSES = K // 512
+WINDOW = 768
+FLOPS = 2 * M * K * T + 2 * K * N * S
+
+TOKEN_CHUNKS = ((0, 256), (256, 384), (384, 512))
+SLOT_CHUNKS = (((0, 512), (512, 768), (768, 1024)), ((0, 512), (512, 768), (768, 896), (896, 1024)))
+PICKED_TAG = {(0, 0): "p00", (0, 512): "p01", (0, 768): "wu_raw11", (1, 0): "p10", (1, 512): "wu_raw11", (1, 768): "p10", (1, 896): "wu_raw11"}
+OUT_CHUNKS = ((0, 256), (256, 512))
+
+
+def tile_moe_prv_lin_bias_kernel(tc, uT, wu, w_words, w_scales, b, gate, offs, pos1, pos2, out):
+    nc = tc.nc
+    with ExitStack() as ctx:
+        keep = ctx.enter_context(tc.tile_pool(name="keep", bufs=1))
+        psum = ctx.enter_context(tc.psum_pool(name="psum", bufs=8))
+
+        offs_sb = keep.tile([P, S // 16], U16, name="offs_sb")
+        pos1_sb = keep.tile([P, T // 16], U16, name="pos1_sb")
+        pos2_sb = keep.tile([P, T // 16], U16, name="pos2_sb")
+
+        w_plane = keep.tile([P, E * PASSES * N], U8, name="w_plane", align_bytes=64)
+        nc.gpsimd.memset(w_plane[:].bitcast(I32), 0)
+        pairs = [[keep.tile([P, WINDOW], U32, name=f"pairs{a}{h}", align_bytes=64) for h in range(2)] for a in range(PASSES)]
+        for a in range(PASSES):
+            for h in range(2):
+                nc.gpsimd.memset(pairs[a][h][:, T:WINDOW], 0)
+
+        wu_rows = wu.rearrange("(p j) c -> p j c", j=4)
+        uT_rows = uT.rearrange("(p j) t -> p j t", j=4)
+        wu_raw = [[keep.tile([P, 4, 256], F32, name=f"wu_raw{a}{c}", tag=f"wu_raw{a}{c}", align_bytes=64) for c in range(2)] for a in range(PASSES)]
+        u_raw = [keep.tile([P, 4, hi - lo], F32, name=f"u_raw{lo}", tag=f"u_raw{lo}", align_bytes=64) for lo, hi in TOKEN_CHUNKS]
+        for c in range(2):
+            nc.sync.dma_start(out=wu_raw[0][c][:], in_=wu_rows[:, :, 256 * c:256 * (c + 1)])
+        for i, (lo, hi) in enumerate(TOKEN_CHUNKS):
+            nc.sync.dma_start(out=u_raw[i][:], in_=uT_rows[:, :, lo:hi])
+        nc.sync.dma_start(offs_sb[:], offs)
+        for c in range(2):
+            nc.sync.dma_start(out=wu_raw[1][c][:], in_=wu_rows[:, :, 512 + 256 * c:512 + 256 * (c + 1)])
+        scale_rows = w_scales.rearrange("e a (q r) n -> r q (e a) n", r=4)
+        for r in range(4):
+            nc.sync.dma_start(
+                out=w_plane[r:P:32, :].bitcast(I32).rearrange("q (g n) -> q g n", n=N // 4),
+                in_=scale_rows[r].bitcast(I32),
+            )
+        w_codes = [keep.tile([P, 4 * PASSES, N], I32, name=f"w_codes{g}", align_bytes=64) for g in range(2)]
+        word_rows = w_words.rearrange("e a p n r -> p (e a) (n r)")
+        for g in range(2):
+            nc.sync.dma_start(out=w_codes[g][:], in_=word_rows[:, 8 * g:8 * (g + 1), :].bitcast(I32))
+        b_sb = keep.tile([P, E], F32, name="b_sb")
+        nc.sync.dma_start(out=b_sb[:], in_=b)
+        gate_sb = [keep.tile([P, T], F32, name=f"gate_sb{r}") for r in range(2)]
+        for r in range(2):
+            nc.sync.dma_start(out=gate_sb[r][:], in_=gate[r])
+        nc.sync.dma_start(pos1_sb[:], pos1)
+        nc.sync.dma_start(pos2_sb[:], pos2)
+
+        warm = keep.tile([P, 2], F32, name="warm")
+        nc.vector.memset(warm[:, 0:1], 0.0)
+        nc.scalar.activation(out=warm[:, 1:2], in_=warm[:, 0:1], func=IDENT)
+
+        wu_bf = [keep.tile([P, 4, P, 4], BF16, name=f"wu_bf{a}", align_bytes=64) for a in range(PASSES)]
+        wu_codes = {}
+        wu_plane = {}
+        u_bf = [keep.tile([P, hi - lo, 4], BF16, name=f"u_bf{lo}", align_bytes=64) for lo, hi in TOKEN_CHUNKS]
+        u_codes = keep.tile([P, T], U32, name="u_codes", align_bytes=64)
+        u_plane = keep.tile([P, T], U8, name="u_plane", align_bytes=64)
+
+        def cast_wu(a, c, copy, lo=0, hi=64):
+            copy(
+                out=wu_bf[a][:, :, 64 * c + lo:64 * c + hi, :].rearrange("p t m j -> p m j t"),
+                in_=wu_raw[a][c][:, :, 4 * lo:4 * hi].rearrange("p j (m t) -> p m j t", t=4),
+            )
+
+        def quantize_wu(a, h):
+            tag = "u_raw384" if (a, h) == (0, 1) else f"wu_codes{a}{h}"
+            wu_codes[(a, h)] = keep.tile([P, 256], U32, name=f"wu_codes{a}{h}", tag=tag, align_bytes=64)
+            wu_plane[(a, h)] = keep.tile([P, 256], U8, name=f"wu_plane{a}{h}", align_bytes=64)
+            nc.vector.quantize_mx(
+                out=wu_codes[(a, h)][:].bitcast(FP8X4),
+                scales=wu_plane[(a, h)][:],
+                in_=wu_bf[a][:, 2 * h:2 * h + 2, :, :].rearrange("p t m j -> p (t m j)"),
+            )
+
+        def cast_u(i, copy, lo=0, hi=128):
+            copy(
+                out=u_bf[i][:, lo:hi, :].rearrange("p (c i) j -> p c j i", i=4),
+                in_=u_raw[i][:, :, lo:hi].rearrange("p j (c i) -> p c j i", i=4),
+            )
+
+        def quantize_u(i):
+            lo, hi = TOKEN_CHUNKS[i]
+            nc.vector.quantize_mx(
+                out=u_codes[:, lo:hi].bitcast(FP8X4),
+                scales=u_plane[:, lo:hi],
+                in_=u_bf[i][:].rearrange("p n j -> p (n j)"),
+            )
+
+        def project(a, h, lo, hi, copy):
+            bank = psum.tile([P, 512], F32, name="bank")
+            acc = bank[:, 0:2 * (hi - lo)].rearrange("p (e n) -> p e n", e=2)
+            for e in range(2):
+                cols = slice(P * e, P * (e + 1))
+                nc.tensor.matmul_mx(
+                    out=acc[:, e, :],
+                    lhsT=wu_codes[(a, h)][:, cols].bitcast(FP8X4), lhsT_scale=wu_plane[(a, h)][:, cols],
+                    rhs=u_codes[:, lo:hi].bitcast(FP8X4), rhs_scale=u_plane[:, lo:hi],
+                    start=True, stop=True,
+                )
+            copy(
+                out=pairs[a][h][:, lo:hi].bitcast(BF16).rearrange("p (n e) -> p n e", e=2),
+                in_=acc.rearrange("p e n -> p n e"),
+            )
+
+        picked = {}
+        x_codes = {}
+        x_plane = {}
+
+        def gather(a, lo, hi, h):
+            if (a, lo) not in picked:
+                picked[(a, lo)] = keep.tile([P, 2, hi - lo], U32, name=f"picked{a}_{lo}", tag=PICKED_TAG[(a, lo)], align_bytes=64)
+            nc.vector.tensor_copy(picked[(a, lo)][:, h, :], pairs[a][h][:].indirect(offs_sb[:, lo // 16:hi // 16]))
+
+        woven = {}
+
+        def weave(a, lo, hi):
+            woven[(a, lo)] = keep.tile([P, hi - lo, 2], U32, name=f"woven{a}_{lo}", align_bytes=64)
+            nc.scalar.copy(out=woven[(a, lo)][:], in_=picked[(a, lo)][:].rearrange("p h n -> p n h"))
+
+        def gather_woven(a, lo, hi):
+            woven[(a, lo)] = keep.tile([P, hi - lo, 2], U32, name=f"woven{a}_{lo}", tag=PICKED_TAG[(a, lo)], align_bytes=64)
+            for h in range(2):
+                nc.vector.tensor_copy(woven[(a, lo)][:, :, h], pairs[a][h][:].indirect(offs_sb[:, lo // 16:hi // 16]))
+
+        def quantize_x(a, lo, hi):
+            codes = keep.tile([P, hi - lo], U32, name=f"x_codes{a}_{lo}", align_bytes=64)
+            plane = keep.tile([P, hi - lo], U8, name=f"x_plane{a}_{lo}", align_bytes=64)
+            nc.vector.quantize_mx(
+                out=codes[:].bitcast(FP8X4), scales=plane[:],
+                in_=woven[(a, lo)][:].rearrange("p n h -> p (n h)").bitcast(BF16),
+            )
+            for e in range(lo // C, hi // C):
+                x_codes[(a, e)] = codes[:, e * C - lo:(e + 1) * C - lo]
+                x_plane[(a, e)] = plane[:, e * C - lo:(e + 1) * C - lo]
+
+        y_sb = keep.tile([P, S], F32, name="y_sb")
+
+        def expert(e):
+            bank = psum.tile([P, 512], F32, name="bank")
+            for a in range(PASSES):
+                g = e * PASSES + a
+                nc.tensor.matmul_mx(
+                    out=bank[:, 0:C],
+                    lhsT=w_codes[g // 8][:, g % 8, :].bitcast(FP8X4), lhsT_scale=w_plane[:, g * N:(g + 1) * N],
+                    rhs=x_codes[(a, e)].bitcast(FP8X4), rhs_scale=x_plane[(a, e)],
+                    start=(a == 0), stop=(a == PASSES - 1),
+                )
+            nc.scalar.activation(out=y_sb[:, e * C:(e + 1) * C], in_=bank[:, 0:C], func=IDENT, bias=b_sb[:, e:e + 1])
+
+        v_copy, s_copy = nc.vector.tensor_copy, nc.scalar.copy
+
+        cast_wu(0, 0, v_copy)
+        cast_wu(0, 1, v_copy, 0, 40)
+        cast_wu(0, 1, s_copy, 40, 64)
+        quantize_wu(0, 0)
+        cast_u(0, v_copy, 0, 168)
+        cast_u(0, s_copy, 168, 256)
+        quantize_u(0)
+        cast_u(1, s_copy)
+        cast_u(2, v_copy)
+        quantize_u(1)
+        quantize_u(2)
+        quantize_wu(0, 1)
+        for h in range(2):
+            for lo, hi in TOKEN_CHUNKS:
+                project(0, h, lo, hi, v_copy if (h, hi) == (0, T) else s_copy)
+        for c in range(2):
+            cast_wu(1, c, s_copy)
+        for lo, hi in SLOT_CHUNKS[0][:2]:
+            for h in range(2):
+                gather(0, lo, hi, h)
+        for h in range(2):
+            quantize_wu(1, h)
+        for h in range(2):
+            gather(0, 768, 1024, h)
+        for h in range(2):
+            for lo, hi in ((0, 256), (256, 512)):
+                project(1, h, lo, hi, s_copy)
+        weave(0, 0, 512)
+        quantize_x(0, 0, 512)
+        for h in range(2):
+            gather(1, 0, 512, h)
+        for lo, hi in SLOT_CHUNKS[0][1:]:
+            weave(0, lo, hi)
+            quantize_x(0, lo, hi)
+        chunks = SLOT_CHUNKS[1]
+        for i, (lo, hi) in enumerate(chunks):
+            if i + 1 < len(chunks):
+                weave(1, lo, hi)
+            quantize_x(1, lo, hi)
+            if i + 2 < len(chunks):
+                for h in range(2):
+                    gather(1, chunks[i + 1][0], chunks[i + 1][1], h)
+            elif i + 1 < len(chunks):
+                gather_woven(1, chunks[i + 1][0], chunks[i + 1][1])
+            for e in range(lo // C, hi // C):
+                expert(e)
+
+        first = keep.tile([P, T], F32, name="first")
+        nc.vector.tensor_tensor(first[:], y_sb[:].indirect(pos1_sb[:]), gate_sb[0][:], MULT)
+        second = [keep.tile([P, hi - lo], F32, name=f"second{lo}") for lo, hi in OUT_CHUNKS]
+        for i, (lo, hi) in enumerate(OUT_CHUNKS):
+            nc.vector.tensor_tensor(second[i][:], y_sb[:].indirect(pos2_sb[:, lo // 16:hi // 16]), gate_sb[1][:, lo:hi], MULT)
+        for i, (lo, hi) in enumerate(OUT_CHUNKS):
+            total = keep.tile([P, hi - lo], F32, name=f"total{lo}")
+            nc.vector.tensor_tensor(total[:], first[:, lo:hi], second[i][:], ADD)
+            (nc.sync, nc.scalar)[i].dma_start(out=out[:, lo:hi], in_=total[:])

@@ -21,8 +21,6 @@ WINDOW = 768
 FLOPS = 2 * M * K * T + 2 * K * N * S
 
 TOKEN_CHUNKS = ((0, 256), (256, 384), (384, 512))
-SLOT_CHUNKS = (((0, 512), (512, 768), (768, 1024)), ((0, 512), (512, 768), (768, 896), (896, 1024)))
-PICKED_TAG = {(0, 0): "p00", (0, 512): "p01", (0, 768): "wu_raw11", (1, 0): "p10", (1, 512): "wu_raw11", (1, 768): "p10", (1, 896): "wu_raw11"}
 OUT_CHUNKS = ((0, 256), (256, 512))
 
 
@@ -37,11 +35,11 @@ def tile_moe_prv_lin_bias_kernel(tc, uT, wu, w_words, w_scales, b, gate, offs, p
         pos2_sb = keep.tile([P, T // 16], U16, name="pos2_sb")
 
         w_plane = keep.tile([P, E * PASSES * N], U8, name="w_plane", align_bytes=64)
-        nc.gpsimd.memset(w_plane[:].bitcast(I32), 0)
+        nc.vector.memset(w_plane[:].bitcast(I32), 0)
         pairs = [[keep.tile([P, WINDOW], U32, name=f"pairs{a}{h}", align_bytes=64) for h in range(2)] for a in range(PASSES)]
         for a in range(PASSES):
             for h in range(2):
-                nc.gpsimd.memset(pairs[a][h][:, T:WINDOW], 0)
+                nc.vector.memset(pairs[a][h][:, T:WINDOW], 0)
 
         wu_rows = wu.rearrange("(p j) c -> p j c", j=4)
         uT_rows = uT.rearrange("(p j) t -> p j t", j=4)
@@ -76,28 +74,33 @@ def tile_moe_prv_lin_bias_kernel(tc, uT, wu, w_words, w_scales, b, gate, offs, p
         nc.vector.memset(warm[:, 0:1], 0.0)
         nc.scalar.activation(out=warm[:, 1:2], in_=warm[:, 0:1], func=IDENT)
 
-        wu_bf = [keep.tile([P, 4, P, 4], BF16, name=f"wu_bf{a}", align_bytes=64) for a in range(PASSES)]
+        stage = keep.tile([P, 2816], U32, name="stage", align_bytes=64)
+        wu_bf = [
+            keep.tile([P, 4, P, 4], BF16, name="wu_bf0", align_bytes=64)[:],
+            stage[:, 1792:2816].bitcast(BF16).rearrange("p (t m j) -> p t m j", t=4, j=4),
+        ]
         wu_codes = {}
         wu_plane = {}
         u_bf = [keep.tile([P, hi - lo, 4], BF16, name=f"u_bf{lo}", align_bytes=64) for lo, hi in TOKEN_CHUNKS]
         u_codes = keep.tile([P, T], U32, name="u_codes", align_bytes=64)
         u_plane = keep.tile([P, T], U8, name="u_plane", align_bytes=64)
 
-        def cast_wu(a, c, copy, lo=0, hi=64):
+        def cast_wu(a, c, copy, lo=0, hi=64, t0=0, t1=4):
             copy(
-                out=wu_bf[a][:, :, 64 * c + lo:64 * c + hi, :].rearrange("p t m j -> p m j t"),
-                in_=wu_raw[a][c][:, :, 4 * lo:4 * hi].rearrange("p j (m t) -> p m j t", t=4),
+                out=wu_bf[a][:, t0:t1, 64 * c + lo:64 * c + hi, :].rearrange("p t m j -> p m j t"),
+                in_=wu_raw[a][c][:, :, 4 * lo:4 * hi].rearrange("p j (m t) -> p m j t", t=4)[:, :, :, t0:t1],
             )
 
         def quantize_wu(a, h):
             tag = "u_raw384" if (a, h) == (0, 1) else f"wu_codes{a}{h}"
             wu_codes[(a, h)] = keep.tile([P, 256], U32, name=f"wu_codes{a}{h}", tag=tag, align_bytes=64)
             wu_plane[(a, h)] = keep.tile([P, 256], U8, name=f"wu_plane{a}{h}", align_bytes=64)
-            nc.vector.quantize_mx(
-                out=wu_codes[(a, h)][:].bitcast(FP8X4),
-                scales=wu_plane[(a, h)][:],
-                in_=wu_bf[a][:, 2 * h:2 * h + 2, :, :].rearrange("p t m j -> p (t m j)"),
-            )
+            for t0, t1 in (((0, 2),), ((0, 1), (1, 2)))[a]:
+                nc.vector.quantize_mx(
+                    out=wu_codes[(a, h)][:, P * t0:P * t1].bitcast(FP8X4),
+                    scales=wu_plane[(a, h)][:, P * t0:P * t1],
+                    in_=wu_bf[a][:, 2 * h + t0:2 * h + t1, :, :].rearrange("p t m j -> p (t m j)"),
+                )
 
         def cast_u(i, copy, lo=0, hi=128):
             copy(
@@ -129,32 +132,24 @@ def tile_moe_prv_lin_bias_kernel(tc, uT, wu, w_words, w_scales, b, gate, offs, p
                 in_=acc.rearrange("p e n -> p n e"),
             )
 
-        picked = {}
         x_codes = {}
         x_plane = {}
 
-        def gather(a, lo, hi, h):
-            if (a, lo) not in picked:
-                picked[(a, lo)] = keep.tile([P, 2, hi - lo], U32, name=f"picked{a}_{lo}", tag=PICKED_TAG[(a, lo)], align_bytes=64)
-            nc.vector.tensor_copy(picked[(a, lo)][:, h, :], pairs[a][h][:].indirect(offs_sb[:, lo // 16:hi // 16]))
+        def gather(place, a, h, lo, hi, skip=0):
+            tile, start, step = place
+            first = start + h * step + skip
+            nc.vector.tensor_copy(tile[:, first:first + hi - lo], pairs[a][h][:].indirect(offs_sb[:, lo // 16:hi // 16]))
 
-        woven = {}
+        def weave(woven, place, copy, lo, hi):
+            tile, start, step = place
+            copy(out=woven, in_=tile[:, start:start + 2 * step].rearrange("p (h n) -> p n h", h=2)[:, lo:hi, :])
 
-        def weave(a, lo, hi):
-            woven[(a, lo)] = keep.tile([P, hi - lo, 2], U32, name=f"woven{a}_{lo}", align_bytes=64)
-            nc.scalar.copy(out=woven[(a, lo)][:], in_=picked[(a, lo)][:].rearrange("p h n -> p n h"))
-
-        def gather_woven(a, lo, hi):
-            woven[(a, lo)] = keep.tile([P, hi - lo, 2], U32, name=f"woven{a}_{lo}", tag=PICKED_TAG[(a, lo)], align_bytes=64)
-            for h in range(2):
-                nc.vector.tensor_copy(woven[(a, lo)][:, :, h], pairs[a][h][:].indirect(offs_sb[:, lo // 16:hi // 16]))
-
-        def quantize_x(a, lo, hi):
+        def quantize_x(woven, a, lo, hi):
             codes = keep.tile([P, hi - lo], U32, name=f"x_codes{a}_{lo}", align_bytes=64)
             plane = keep.tile([P, hi - lo], U8, name=f"x_plane{a}_{lo}", align_bytes=64)
             nc.vector.quantize_mx(
                 out=codes[:].bitcast(FP8X4), scales=plane[:],
-                in_=woven[(a, lo)][:].rearrange("p n h -> p (n h)").bitcast(BF16),
+                in_=woven[:].rearrange("p n h -> p (n h)").bitcast(BF16),
             )
             for e in range(lo // C, hi // C):
                 x_codes[(a, e)] = codes[:, e * C - lo:(e + 1) * C - lo]
@@ -188,40 +183,57 @@ def tile_moe_prv_lin_bias_kernel(tc, uT, wu, w_words, w_scales, b, gate, offs, p
         quantize_u(1)
         quantize_u(2)
         quantize_wu(0, 1)
-        for h in range(2):
-            for lo, hi in TOKEN_CHUNKS:
-                project(0, h, lo, hi, v_copy if (h, hi) == (0, T) else s_copy)
-        for c in range(2):
-            cast_wu(1, c, s_copy)
-        for lo, hi in SLOT_CHUNKS[0][:2]:
-            for h in range(2):
-                gather(0, lo, hi, h)
-        for h in range(2):
-            quantize_wu(1, h)
-        for h in range(2):
-            gather(0, 768, 1024, h)
-        for h in range(2):
-            for lo, hi in ((0, 256), (256, 512)):
-                project(1, h, lo, hi, s_copy)
-        weave(0, 0, 512)
-        quantize_x(0, 0, 512)
-        for h in range(2):
-            gather(1, 0, 512, h)
-        for lo, hi in SLOT_CHUNKS[0][1:]:
-            weave(0, lo, hi)
-            quantize_x(0, lo, hi)
-        chunks = SLOT_CHUNKS[1]
-        for i, (lo, hi) in enumerate(chunks):
-            if i + 1 < len(chunks):
-                weave(1, lo, hi)
-            quantize_x(1, lo, hi)
-            if i + 2 < len(chunks):
-                for h in range(2):
-                    gather(1, chunks[i + 1][0], chunks[i + 1][1], h)
-            elif i + 1 < len(chunks):
-                gather_woven(1, chunks[i + 1][0], chunks[i + 1][1])
+        project(0, 0, 0, 256, s_copy)
+        project(0, 0, 256, 384, v_copy)
+        project(0, 0, 384, 512, v_copy)
+        cast_wu(1, 0, s_copy)
+        project(0, 1, 0, 256, s_copy)
+        project(0, 1, 256, 512, s_copy)
+        cast_wu(1, 1, s_copy, 0, 64, 0, 2)
+        cast_wu(1, 1, s_copy, 0, 64, 2, 4)
+
+        p0 = (stage, 512, 1024)
+        stage_a = keep.tile([P, 768], U32, name="stage_a", align_bytes=64)
+        picked = [(stage_a, 256, 256), (stage, 256, 768), (stage_a, 0, 256), (stage, 0, 256)]
+        gather(p0, 0, 0, 0, 512)
+        gather(p0, 0, 0, 512, 1024, 512)
+        gather(p0, 0, 1, 0, 256)
+        quantize_wu(1, 0)
+        gather(p0, 0, 1, 256, 512, 256)
+        quantize_wu(1, 1)
+        gather(p0, 0, 1, 512, 1024, 512)
+        w0a = keep.tile([P, 512, 2], U32, name="w0a", align_bytes=64)
+        weave(w0a[:, 0:256, :], p0, s_copy, 0, 256)
+        for lo, hi in ((0, 256), (256, 512)):
+            project(1, 0, lo, hi, s_copy)
+        weave(w0a[:, 256:512, :], p0, s_copy, 256, 512)
+        for lo, hi in ((0, 256), (256, 512)):
+            project(1, 1, lo, hi, s_copy)
+        for i in range(4):
+            gather(picked[i], 1, 0, 256 * i, 256 * (i + 1))
+        w0b = keep.tile([P, 512, 2], U32, name="w0b", align_bytes=64)
+        weave(w0b[:], p0, s_copy, 512, 1024)
+        quantize_x(w0a, 0, 0, 512)
+        gather(picked[0], 1, 1, 0, 256)
+        quantize_x(w0b, 0, 512, 1024)
+        gather(picked[1], 1, 1, 256, 512)
+        for i in range(3):
+            lo, hi = 256 * i, 256 * (i + 1)
+            woven = keep.tile([P, 256, 2], U32, name=f"w1_{i}", align_bytes=64)
+            weave(woven[:], picked[i], s_copy, 0, 256)
+            quantize_x(woven, 1, lo, hi)
+            if i < 2:
+                gather(picked[i + 2], 1, 1, lo + 512, hi + 512)
+            else:
+                last = [keep.tile([P, C, 2], U32, name=f"w1_last{j}", align_bytes=64) for j in range(2)]
+                weave(last[0][:], picked[3], s_copy, 0, C)
+                weave(last[1][:], picked[3], v_copy, C, 2 * C)
             for e in range(lo // C, hi // C):
                 expert(e)
+        for j in range(2):
+            quantize_x(last[j], 1, 768 + C * j, 768 + C * (j + 1))
+        for e in range(6, 8):
+            expert(e)
 
         first = keep.tile([P, T], F32, name="first")
         nc.vector.tensor_tensor(first[:], y_sb[:].indirect(pos1_sb[:]), gate_sb[0][:], MULT)

@@ -17,7 +17,7 @@ K, T, E, C, N, M = 1024, 512, 8, 128, 128, 512
 P = 128
 S = E * C
 PASSES = K // 512
-WINDOW = 768
+WINDOWS = (1408, 768)
 FLOPS = 2 * M * K * T + 2 * K * N * S
 
 TOKEN_CHUNKS = ((0, 256), (256, 384), (384, 512))
@@ -34,12 +34,16 @@ def tile_moe_prv_lin_bias_kernel(tc, uT, wu, w_words, w_scales, b, gate, offs, p
         pos1_sb = keep.tile([P, T // 16], U16, name="pos1_sb")
         pos2_sb = keep.tile([P, T // 16], U16, name="pos2_sb")
 
+        warm = keep.tile([P, 2], F32, name="warm")
+        nc.vector.memset(warm[:, 0:1], 0.0)
+        nc.scalar.activation(out=warm[:, 1:2], in_=warm[:, 0:1], func=IDENT)
+
         w_plane = keep.tile([P, E * PASSES * N], U8, name="w_plane", align_bytes=64)
         nc.vector.memset(w_plane[:].bitcast(I32), 0)
-        pairs = [[keep.tile([P, WINDOW], U32, name=f"pairs{a}{h}", align_bytes=64) for h in range(2)] for a in range(PASSES)]
+        pairs = [[keep.tile([P, WINDOWS[h]], U32, name=f"pairs{a}{h}", align_bytes=64) for h in range(2)] for a in range(PASSES)]
         for a in range(PASSES):
             for h in range(2):
-                nc.vector.memset(pairs[a][h][:, T:WINDOW], 0)
+                nc.vector.memset(pairs[a][h][:, T:WINDOWS[h]], 0)
 
         wu_rows = wu.rearrange("(p j) c -> p j c", j=4)
         uT_rows = uT.rearrange("(p j) t -> p j t", j=4)
@@ -70,14 +74,10 @@ def tile_moe_prv_lin_bias_kernel(tc, uT, wu, w_words, w_scales, b, gate, offs, p
         nc.sync.dma_start(pos1_sb[:], pos1)
         nc.sync.dma_start(pos2_sb[:], pos2)
 
-        warm = keep.tile([P, 2], F32, name="warm")
-        nc.vector.memset(warm[:, 0:1], 0.0)
-        nc.scalar.activation(out=warm[:, 1:2], in_=warm[:, 0:1], func=IDENT)
-
-        stage = keep.tile([P, 2816], U32, name="stage", align_bytes=64)
+        stage = keep.tile([P, 3584], U32, name="stage", align_bytes=64)
         wu_bf = [
             keep.tile([P, 4, P, 4], BF16, name="wu_bf0", align_bytes=64)[:],
-            stage[:, 1792:2816].bitcast(BF16).rearrange("p (t m j) -> p t m j", t=4, j=4),
+            stage[:, 2560:3584].bitcast(BF16).rearrange("p (t m j) -> p t m j", t=4, j=4),
         ]
         wu_codes = {}
         wu_plane = {}
@@ -192,11 +192,9 @@ def tile_moe_prv_lin_bias_kernel(tc, uT, wu, w_words, w_scales, b, gate, offs, p
         cast_wu(1, 1, s_copy, 0, 64, 0, 2)
         cast_wu(1, 1, s_copy, 0, 64, 2, 4)
 
-        p0 = (stage, 512, 1024)
-        stage_a = keep.tile([P, 768], U32, name="stage_a", align_bytes=64)
-        picked = [(stage_a, 256, 256), (stage, 256, 768), (stage_a, 0, 256), (stage, 0, 256)]
-        gather(p0, 0, 0, 0, 512)
-        gather(p0, 0, 0, 512, 1024, 512)
+        p0 = (stage, 1280, 1024)
+        picked = [(stage, 0, 1024), (stage, 256, 1536), (stage, 512, 512), (stage, 768, 1024)]
+        gather(p0, 0, 0, 0, 1024)
         gather(p0, 0, 1, 0, 256)
         quantize_wu(1, 0)
         gather(p0, 0, 1, 256, 512, 256)
@@ -209,8 +207,7 @@ def tile_moe_prv_lin_bias_kernel(tc, uT, wu, w_words, w_scales, b, gate, offs, p
         weave(w0a[:, 256:512, :], p0, s_copy, 256, 512)
         for lo, hi in ((0, 256), (256, 512)):
             project(1, 1, lo, hi, s_copy)
-        for i in range(4):
-            gather(picked[i], 1, 0, 256 * i, 256 * (i + 1))
+        gather(picked[0], 1, 0, 0, 1024)
         w0b = keep.tile([P, 512, 2], U32, name="w0b", align_bytes=64)
         weave(w0b[:], p0, s_copy, 512, 1024)
         quantize_x(w0a, 0, 0, 512)

@@ -75,10 +75,7 @@ def tile_moe_prv_lin_bias_kernel(tc, uT, wu, w_words, w_scales, b, gate, offs, p
         nc.sync.dma_start(pos2_sb[:], pos2)
 
         stage = keep.tile([P, 3584], U32, name="stage", align_bytes=64)
-        wu_bf = [
-            keep.tile([P, 4, P, 4], BF16, name="wu_bf0", align_bytes=64)[:],
-            stage[:, 2560:3584].bitcast(BF16).rearrange("p (t m j) -> p t m j", t=4, j=4),
-        ]
+        wu_bf = 2 * [stage[:, 2560:3584].bitcast(BF16).rearrange("p (t m j) -> p t m j", t=4, j=4)]
         wu_codes = {}
         wu_plane = {}
         u_bf = [keep.tile([P, hi - lo, 4], BF16, name=f"u_bf{lo}", align_bytes=64) for lo, hi in TOKEN_CHUNKS]
@@ -144,6 +141,9 @@ def tile_moe_prv_lin_bias_kernel(tc, uT, wu, w_words, w_scales, b, gate, offs, p
             tile, start, step = place
             copy(out=woven, in_=tile[:, start:start + 2 * step].rearrange("p (h n) -> p n h", h=2)[:, lo:hi, :])
 
+        def g_cast(out, in_):
+            nc.gpsimd.tensor_scalar(out.rearrange("p m j t -> p m t j"), in_.rearrange("p m j t -> p m t j"), 1.0, 0.0, MULT, ADD)
+
         def quantize_x(woven, a, lo, hi):
             codes = keep.tile([P, hi - lo], U32, name=f"x_codes{a}_{lo}", align_bytes=64)
             plane = keep.tile([P, hi - lo], U8, name=f"x_plane{a}_{lo}", align_bytes=64)
@@ -185,8 +185,8 @@ def tile_moe_prv_lin_bias_kernel(tc, uT, wu, w_words, w_scales, b, gate, offs, p
         quantize_wu(0, 1)
         project(0, 0, 0, 256, s_copy)
         project(0, 0, 256, 384, v_copy)
-        project(0, 0, 384, 512, v_copy)
-        cast_wu(1, 0, s_copy)
+        project(0, 0, 384, 512, s_copy)
+        cast_wu(1, 0, g_cast)
         project(0, 1, 0, 256, s_copy)
         project(0, 1, 256, 512, s_copy)
         cast_wu(1, 1, s_copy, 0, 64, 0, 2)
@@ -195,16 +195,14 @@ def tile_moe_prv_lin_bias_kernel(tc, uT, wu, w_words, w_scales, b, gate, offs, p
         p0 = (stage, 1280, 1024)
         picked = [(stage, 0, 1024), (stage, 256, 1536), (stage, 512, 512), (stage, 768, 1024)]
         gather(p0, 0, 0, 0, 1024)
-        gather(p0, 0, 1, 0, 256)
         quantize_wu(1, 0)
-        gather(p0, 0, 1, 256, 512, 256)
+        gather(p0, 0, 1, 0, 512)
         quantize_wu(1, 1)
         gather(p0, 0, 1, 512, 1024, 512)
-        w0a = keep.tile([P, 512, 2], U32, name="w0a", align_bytes=64)
-        weave(w0a[:, 0:256, :], p0, s_copy, 0, 256)
+        w0a = keep.tile([P, 512, 2], U32, name="w0a", tag="wu_codes10", align_bytes=64)
         for lo, hi in ((0, 256), (256, 512)):
             project(1, 0, lo, hi, s_copy)
-        weave(w0a[:, 256:512, :], p0, s_copy, 256, 512)
+        weave(w0a[:], p0, s_copy, 0, 512)
         for lo, hi in ((0, 256), (256, 512)):
             project(1, 1, lo, hi, s_copy)
         gather(picked[0], 1, 0, 0, 1024)

@@ -17,18 +17,33 @@ K, T, E, C, N, M = 1024, 512, 8, 128, 128, 512
 P = 128
 S = E * C
 PASSES = K // 512
-WINDOWS = (1408, 768)
 FLOPS = 2 * M * K * T + 2 * K * N * S
 
+BANKS = 8
+BANK = 512
+WU_LOAD = 256
+QUADS = WU_LOAD // 4
+HALF = S // 2
+QUARTER = S // 4
+WINDOWS = (1408, 768)
 TOKEN_CHUNKS = ((0, 256), (256, 384), (384, 512))
-OUT_CHUNKS = ((0, 256), (256, 512))
+TOKEN_HALVES = ((0, 256), (256, 512))
+WU_VECTOR_SHARE = 40
+U_VECTOR_SHARE = 168
+
+FIRST_1 = 0
+SPARE_1 = FIRST_1 + S
+FIRST_0 = SPARE_1 + QUARTER
+ROUNDED_WU = FIRST_0 + S + QUARTER
+STAGE_WORDS = ROUNDED_WU + 1024
+SECOND_1 = (SPARE_1, FIRST_0 + HALF, SPARE_1, FIRST_0 + HALF)
 
 
 def tile_moe_prv_lin_bias_kernel(tc, uT, wu, w_words, w_scales, b, gate, offs, pos1, pos2, out):
     nc = tc.nc
     with ExitStack() as ctx:
         keep = ctx.enter_context(tc.tile_pool(name="keep", bufs=1))
-        psum = ctx.enter_context(tc.psum_pool(name="psum", bufs=8))
+        psum = ctx.enter_context(tc.psum_pool(name="psum", bufs=BANKS))
 
         offs_sb = keep.tile([P, S // 16], U16, name="offs_sb")
         pos1_sb = keep.tile([P, T // 16], U16, name="pos1_sb")
@@ -38,8 +53,8 @@ def tile_moe_prv_lin_bias_kernel(tc, uT, wu, w_words, w_scales, b, gate, offs, p
         nc.vector.memset(warm[:, 0:1], 0.0)
         nc.scalar.activation(out=warm[:, 1:2], in_=warm[:, 0:1], func=IDENT)
 
-        w_plane = keep.tile([P, E * PASSES * N], U8, name="w_plane", align_bytes=64)
-        nc.vector.memset(w_plane[:].bitcast(I32), 0)
+        w_scale_sb = keep.tile([P, E * PASSES * N], U8, name="w_scale_sb", align_bytes=64)
+        nc.vector.memset(w_scale_sb[:].bitcast(I32), 0)
         pairs = [[keep.tile([P, WINDOWS[h]], U32, name=f"pairs{a}{h}", align_bytes=64) for h in range(2)] for a in range(PASSES)]
         for a in range(PASSES):
             for h in range(2):
@@ -47,25 +62,30 @@ def tile_moe_prv_lin_bias_kernel(tc, uT, wu, w_words, w_scales, b, gate, offs, p
 
         wu_rows = wu.rearrange("(p j) c -> p j c", j=4)
         uT_rows = uT.rearrange("(p j) t -> p j t", j=4)
-        wu_raw = [[keep.tile([P, 4, 256], F32, name=f"wu_raw{a}{c}", tag=f"wu_raw{a}{c}", align_bytes=64) for c in range(2)] for a in range(PASSES)]
+        wu_raw = [[keep.tile([P, 4, WU_LOAD], F32, name=f"wu_raw{a}{c}", align_bytes=64) for c in range(2)] for a in range(PASSES)]
         u_raw = [keep.tile([P, 4, hi - lo], F32, name=f"u_raw{lo}", tag=f"u_raw{lo}", align_bytes=64) for lo, hi in TOKEN_CHUNKS]
-        for c in range(2):
-            nc.sync.dma_start(out=wu_raw[0][c][:], in_=wu_rows[:, :, 256 * c:256 * (c + 1)])
+
+        def load_wu(a):
+            for c in range(2):
+                first_column = 512 * a + WU_LOAD * c
+                nc.sync.dma_start(out=wu_raw[a][c][:], in_=wu_rows[:, :, first_column:first_column + WU_LOAD])
+
+        load_wu(0)
         for i, (lo, hi) in enumerate(TOKEN_CHUNKS):
             nc.sync.dma_start(out=u_raw[i][:], in_=uT_rows[:, :, lo:hi])
         nc.sync.dma_start(offs_sb[:], offs)
-        for c in range(2):
-            nc.sync.dma_start(out=wu_raw[1][c][:], in_=wu_rows[:, :, 512 + 256 * c:512 + 256 * (c + 1)])
+        load_wu(1)
         scale_rows = w_scales.rearrange("e a (q r) n -> r q (e a) n", r=4)
         for r in range(4):
             nc.sync.dma_start(
-                out=w_plane[r:P:32, :].bitcast(I32).rearrange("q (g n) -> q g n", n=N // 4),
+                out=w_scale_sb[r:P:32, :].bitcast(I32).rearrange("q (g n) -> q g n", n=N // 4),
                 in_=scale_rows[r].bitcast(I32),
             )
-        w_codes = [keep.tile([P, 4 * PASSES, N], I32, name=f"w_codes{g}", align_bytes=64) for g in range(2)]
+        per_load = E * PASSES // 2
+        w_codes = [keep.tile([P, per_load, N], I32, name=f"w_codes{i}", align_bytes=64) for i in range(2)]
         word_rows = w_words.rearrange("e a p n r -> p (e a) (n r)")
-        for g in range(2):
-            nc.sync.dma_start(out=w_codes[g][:], in_=word_rows[:, 8 * g:8 * (g + 1), :].bitcast(I32))
+        for i in range(2):
+            nc.sync.dma_start(out=w_codes[i][:], in_=word_rows[:, per_load * i:per_load * (i + 1), :].bitcast(I32))
         b_sb = keep.tile([P, E], F32, name="b_sb")
         nc.sync.dma_start(out=b_sb[:], in_=b)
         gate_sb = [keep.tile([P, T], F32, name=f"gate_sb{r}") for r in range(2)]
@@ -74,54 +94,59 @@ def tile_moe_prv_lin_bias_kernel(tc, uT, wu, w_words, w_scales, b, gate, offs, p
         nc.sync.dma_start(pos1_sb[:], pos1)
         nc.sync.dma_start(pos2_sb[:], pos2)
 
-        stage = keep.tile([P, 3584], U32, name="stage", align_bytes=64)
-        wu_bf = 2 * [stage[:, 2560:3584].bitcast(BF16).rearrange("p (t m j) -> p t m j", t=4, j=4)]
+        stage = keep.tile([P, STAGE_WORDS], U32, name="stage", align_bytes=64)
+        wu_bf = stage[:, ROUNDED_WU:STAGE_WORDS].bitcast(BF16).rearrange("p (t m j) -> p t m j", t=4, j=4)
         wu_codes = {}
-        wu_plane = {}
+        wu_scales = {}
         u_bf = [keep.tile([P, hi - lo, 4], BF16, name=f"u_bf{lo}", align_bytes=64) for lo, hi in TOKEN_CHUNKS]
         u_codes = keep.tile([P, T], U32, name="u_codes", align_bytes=64)
-        u_plane = keep.tile([P, T], U8, name="u_plane", align_bytes=64)
+        u_scales = keep.tile([P, T], U8, name="u_scales", align_bytes=64)
 
-        def cast_wu(a, c, copy, lo=0, hi=64, t0=0, t1=4):
+        v_copy, s_copy = nc.vector.tensor_copy, nc.scalar.copy
+
+        def g_copy(out, in_):
+            nc.gpsimd.tensor_scalar(out.rearrange("p m j t -> p m t j"), in_.rearrange("p m j t -> p m t j"), 1.0, 0.0, MULT, ADD)
+
+        def cast_wu(a, c, copy, lo=0, hi=QUADS, t0=0, t1=4):
             copy(
-                out=wu_bf[a][:, t0:t1, 64 * c + lo:64 * c + hi, :].rearrange("p t m j -> p m j t"),
+                out=wu_bf[:, t0:t1, QUADS * c + lo:QUADS * c + hi, :].rearrange("p t m j -> p m j t"),
                 in_=wu_raw[a][c][:, :, 4 * lo:4 * hi].rearrange("p j (m t) -> p m j t", t=4)[:, :, :, t0:t1],
             )
 
-        def quantize_wu(a, h):
-            tag = "u_raw384" if (a, h) == (0, 1) else f"wu_codes{a}{h}"
-            wu_codes[(a, h)] = keep.tile([P, 256], U32, name=f"wu_codes{a}{h}", tag=tag, align_bytes=64)
-            wu_plane[(a, h)] = keep.tile([P, 256], U8, name=f"wu_plane{a}{h}", align_bytes=64)
-            for t0, t1 in (((0, 2),), ((0, 1), (1, 2)))[a]:
+        def quantize_wu(a, h, tag, outputs_a_call):
+            wu_codes[(a, h)] = keep.tile([P, 2 * P], U32, name=f"wu_codes{a}{h}", tag=tag, align_bytes=64)
+            wu_scales[(a, h)] = keep.tile([P, 2 * P], U8, name=f"wu_scales{a}{h}", align_bytes=64)
+            for e0 in range(0, 2, outputs_a_call):
+                e1 = e0 + outputs_a_call
                 nc.vector.quantize_mx(
-                    out=wu_codes[(a, h)][:, P * t0:P * t1].bitcast(FP8X4),
-                    scales=wu_plane[(a, h)][:, P * t0:P * t1],
-                    in_=wu_bf[a][:, 2 * h + t0:2 * h + t1, :, :].rearrange("p t m j -> p (t m j)"),
+                    out=wu_codes[(a, h)][:, P * e0:P * e1].bitcast(FP8X4),
+                    scales=wu_scales[(a, h)][:, P * e0:P * e1],
+                    in_=wu_bf[:, 2 * h + e0:2 * h + e1, :, :].rearrange("p t m j -> p (t m j)"),
                 )
 
         def cast_u(i, copy, lo=0, hi=128):
             copy(
-                out=u_bf[i][:, lo:hi, :].rearrange("p (c i) j -> p c j i", i=4),
-                in_=u_raw[i][:, :, lo:hi].rearrange("p j (c i) -> p c j i", i=4),
+                out=u_bf[i][:, lo:hi, :].rearrange("p (c n) j -> p c j n", n=4),
+                in_=u_raw[i][:, :, lo:hi].rearrange("p j (c n) -> p c j n", n=4),
             )
 
         def quantize_u(i):
             lo, hi = TOKEN_CHUNKS[i]
             nc.vector.quantize_mx(
                 out=u_codes[:, lo:hi].bitcast(FP8X4),
-                scales=u_plane[:, lo:hi],
+                scales=u_scales[:, lo:hi],
                 in_=u_bf[i][:].rearrange("p n j -> p (n j)"),
             )
 
         def project(a, h, lo, hi, copy):
-            bank = psum.tile([P, 512], F32, name="bank")
+            bank = psum.tile([P, BANK], F32, name="bank")
             acc = bank[:, 0:2 * (hi - lo)].rearrange("p (e n) -> p e n", e=2)
             for e in range(2):
                 cols = slice(P * e, P * (e + 1))
                 nc.tensor.matmul_mx(
                     out=acc[:, e, :],
-                    lhsT=wu_codes[(a, h)][:, cols].bitcast(FP8X4), lhsT_scale=wu_plane[(a, h)][:, cols],
-                    rhs=u_codes[:, lo:hi].bitcast(FP8X4), rhs_scale=u_plane[:, lo:hi],
+                    lhsT=wu_codes[(a, h)][:, cols].bitcast(FP8X4), lhsT_scale=wu_scales[(a, h)][:, cols],
+                    rhs=u_codes[:, lo:hi].bitcast(FP8X4), rhs_scale=u_scales[:, lo:hi],
                     start=True, stop=True,
                 )
             copy(
@@ -129,113 +154,103 @@ def tile_moe_prv_lin_bias_kernel(tc, uT, wu, w_words, w_scales, b, gate, offs, p
                 in_=acc.rearrange("p e n -> p n e"),
             )
 
+        def gather(at, a, h, lo, hi):
+            nc.vector.tensor_copy(stage[:, at:at + hi - lo], pairs[a][h][:].indirect(offs_sb[:, lo // 16:hi // 16]))
+
+        def weave(woven, first, second, copy, lo, hi):
+            step = second - first
+            copy(out=woven[:], in_=stage[:, first:first + 2 * step].rearrange("p (h n) -> p n h", h=2)[:, lo:hi, :])
+
         x_codes = {}
-        x_plane = {}
-
-        def gather(place, a, h, lo, hi, skip=0):
-            tile, start, step = place
-            first = start + h * step + skip
-            nc.vector.tensor_copy(tile[:, first:first + hi - lo], pairs[a][h][:].indirect(offs_sb[:, lo // 16:hi // 16]))
-
-        def weave(woven, place, copy, lo, hi):
-            tile, start, step = place
-            copy(out=woven, in_=tile[:, start:start + 2 * step].rearrange("p (h n) -> p n h", h=2)[:, lo:hi, :])
-
-        def g_cast(out, in_):
-            nc.gpsimd.tensor_scalar(out.rearrange("p m j t -> p m t j"), in_.rearrange("p m j t -> p m t j"), 1.0, 0.0, MULT, ADD)
+        x_scales = {}
 
         def quantize_x(woven, a, lo, hi):
             codes = keep.tile([P, hi - lo], U32, name=f"x_codes{a}_{lo}", align_bytes=64)
-            plane = keep.tile([P, hi - lo], U8, name=f"x_plane{a}_{lo}", align_bytes=64)
+            scales = keep.tile([P, hi - lo], U8, name=f"x_scales{a}_{lo}", align_bytes=64)
             nc.vector.quantize_mx(
-                out=codes[:].bitcast(FP8X4), scales=plane[:],
+                out=codes[:].bitcast(FP8X4), scales=scales[:],
                 in_=woven[:].rearrange("p n h -> p (n h)").bitcast(BF16),
             )
             for e in range(lo // C, hi // C):
                 x_codes[(a, e)] = codes[:, e * C - lo:(e + 1) * C - lo]
-                x_plane[(a, e)] = plane[:, e * C - lo:(e + 1) * C - lo]
+                x_scales[(a, e)] = scales[:, e * C - lo:(e + 1) * C - lo]
 
         y_sb = keep.tile([P, S], F32, name="y_sb")
 
         def expert(e):
-            bank = psum.tile([P, 512], F32, name="bank")
+            bank = psum.tile([P, BANK], F32, name="bank")
             for a in range(PASSES):
                 g = e * PASSES + a
                 nc.tensor.matmul_mx(
                     out=bank[:, 0:C],
-                    lhsT=w_codes[g // 8][:, g % 8, :].bitcast(FP8X4), lhsT_scale=w_plane[:, g * N:(g + 1) * N],
-                    rhs=x_codes[(a, e)].bitcast(FP8X4), rhs_scale=x_plane[(a, e)],
+                    lhsT=w_codes[g // per_load][:, g % per_load, :].bitcast(FP8X4), lhsT_scale=w_scale_sb[:, g * N:(g + 1) * N],
+                    rhs=x_codes[(a, e)].bitcast(FP8X4), rhs_scale=x_scales[(a, e)],
                     start=(a == 0), stop=(a == PASSES - 1),
                 )
             nc.scalar.activation(out=y_sb[:, e * C:(e + 1) * C], in_=bank[:, 0:C], func=IDENT, bias=b_sb[:, e:e + 1])
 
-        v_copy, s_copy = nc.vector.tensor_copy, nc.scalar.copy
-
         cast_wu(0, 0, v_copy)
-        cast_wu(0, 1, v_copy, 0, 40)
-        cast_wu(0, 1, s_copy, 40, 64)
-        quantize_wu(0, 0)
-        cast_u(0, v_copy, 0, 168)
-        cast_u(0, s_copy, 168, 256)
+        cast_wu(0, 1, v_copy, 0, WU_VECTOR_SHARE)
+        cast_wu(0, 1, s_copy, WU_VECTOR_SHARE, QUADS)
+        quantize_wu(0, 0, "wu_codes00", 2)
+        cast_u(0, v_copy, 0, U_VECTOR_SHARE)
+        cast_u(0, s_copy, U_VECTOR_SHARE, TOKEN_CHUNKS[0][1])
         quantize_u(0)
         cast_u(1, s_copy)
         cast_u(2, v_copy)
         quantize_u(1)
         quantize_u(2)
-        quantize_wu(0, 1)
-        project(0, 0, 0, 256, s_copy)
-        project(0, 0, 256, 384, v_copy)
-        project(0, 0, 384, 512, s_copy)
-        cast_wu(1, 0, g_cast)
-        project(0, 1, 0, 256, s_copy)
-        project(0, 1, 256, 512, s_copy)
-        cast_wu(1, 1, s_copy, 0, 64, 0, 2)
-        cast_wu(1, 1, s_copy, 0, 64, 2, 4)
+        quantize_wu(0, 1, f"u_raw{TOKEN_CHUNKS[2][0]}", 2)
+        for (lo, hi), copy in zip(TOKEN_CHUNKS, (s_copy, v_copy, s_copy)):
+            project(0, 0, lo, hi, copy)
+        cast_wu(1, 0, g_copy)
+        for lo, hi in TOKEN_HALVES:
+            project(0, 1, lo, hi, s_copy)
+        for h in range(2):
+            cast_wu(1, 1, s_copy, 0, QUADS, 2 * h, 2 * h + 2)
 
-        p0 = (stage, 1280, 1024)
-        picked = [(stage, 0, 1024), (stage, 256, 1536), (stage, 512, 512), (stage, 768, 1024)]
-        gather(p0, 0, 0, 0, 1024)
-        quantize_wu(1, 0)
-        gather(p0, 0, 1, 0, 512)
-        quantize_wu(1, 1)
-        gather(p0, 0, 1, 512, 1024, 512)
-        w0a = keep.tile([P, 512, 2], U32, name="w0a", tag="wu_codes10", align_bytes=64)
-        for lo, hi in ((0, 256), (256, 512)):
+        second_0 = FIRST_0 + S
+        gather(FIRST_0, 0, 0, 0, S)
+        for h in range(2):
+            quantize_wu(1, h, f"wu_codes1{h}", 1)
+            gather(second_0 + HALF * h, 0, 1, HALF * h, HALF * (h + 1))
+        woven_0a = keep.tile([P, HALF, 2], U32, name="woven_0a", tag="wu_codes10", align_bytes=64)
+        for lo, hi in TOKEN_HALVES:
             project(1, 0, lo, hi, s_copy)
-        weave(w0a[:], p0, s_copy, 0, 512)
-        for lo, hi in ((0, 256), (256, 512)):
+        weave(woven_0a, FIRST_0, second_0, s_copy, 0, HALF)
+        for lo, hi in TOKEN_HALVES:
             project(1, 1, lo, hi, s_copy)
-        gather(picked[0], 1, 0, 0, 1024)
-        w0b = keep.tile([P, 512, 2], U32, name="w0b", align_bytes=64)
-        weave(w0b[:], p0, s_copy, 512, 1024)
-        quantize_x(w0a, 0, 0, 512)
-        gather(picked[0], 1, 1, 0, 256)
-        quantize_x(w0b, 0, 512, 1024)
-        gather(picked[1], 1, 1, 256, 512)
+        gather(FIRST_1, 1, 0, 0, S)
+        woven_0b = keep.tile([P, HALF, 2], U32, name="woven_0b", align_bytes=64)
+        weave(woven_0b, FIRST_0, second_0, s_copy, HALF, S)
+
+        for i, woven in enumerate((woven_0a, woven_0b)):
+            gather(SECOND_1[i], 1, 1, QUARTER * i, QUARTER * (i + 1))
+            quantize_x(woven, 0, HALF * i, HALF * (i + 1))
         for i in range(3):
-            lo, hi = 256 * i, 256 * (i + 1)
-            woven = keep.tile([P, 256, 2], U32, name=f"w1_{i}", align_bytes=64)
-            weave(woven[:], picked[i], s_copy, 0, 256)
-            quantize_x(woven, 1, lo, hi)
+            lo, hi = QUARTER * i, QUARTER * (i + 1)
+            woven = keep.tile([P, QUARTER, 2], U32, name=f"woven_1_{i}", align_bytes=64)
+            weave(woven, FIRST_1 + lo, SECOND_1[i], s_copy, 0, QUARTER)
             if i < 2:
-                gather(picked[i + 2], 1, 1, lo + 512, hi + 512)
+                gather(SECOND_1[i + 2], 1, 1, lo + HALF, hi + HALF)
             else:
-                last = [keep.tile([P, C, 2], U32, name=f"w1_last{j}", align_bytes=64) for j in range(2)]
-                weave(last[0][:], picked[3], s_copy, 0, C)
-                weave(last[1][:], picked[3], v_copy, C, 2 * C)
+                last = [keep.tile([P, C, 2], U32, name=f"woven_last{j}", align_bytes=64) for j in range(2)]
+                for j, copy in enumerate((v_copy, s_copy)):
+                    weave(last[j], FIRST_1 + hi, SECOND_1[3], copy, C * j, C * (j + 1))
+            quantize_x(woven, 1, lo, hi)
             for e in range(lo // C, hi // C):
                 expert(e)
         for j in range(2):
-            quantize_x(last[j], 1, 768 + C * j, 768 + C * (j + 1))
-        for e in range(6, 8):
+            quantize_x(last[j], 1, S - QUARTER + C * j, S - QUARTER + C * (j + 1))
+        for e in range(E - 2, E):
             expert(e)
 
         first = keep.tile([P, T], F32, name="first")
         nc.vector.tensor_tensor(first[:], y_sb[:].indirect(pos1_sb[:]), gate_sb[0][:], MULT)
-        second = [keep.tile([P, hi - lo], F32, name=f"second{lo}") for lo, hi in OUT_CHUNKS]
-        for i, (lo, hi) in enumerate(OUT_CHUNKS):
+        second = [keep.tile([P, hi - lo], F32, name=f"second{lo}") for lo, hi in TOKEN_HALVES]
+        for i, (lo, hi) in enumerate(TOKEN_HALVES):
             nc.vector.tensor_tensor(second[i][:], y_sb[:].indirect(pos2_sb[:, lo // 16:hi // 16]), gate_sb[1][:, lo:hi], MULT)
-        for i, (lo, hi) in enumerate(OUT_CHUNKS):
+        for i, (lo, hi) in enumerate(TOKEN_HALVES):
             total = keep.tile([P, hi - lo], F32, name=f"total{lo}")
             nc.vector.tensor_tensor(total[:], first[:, lo:hi], second[i][:], ADD)
             (nc.sync, nc.scalar)[i].dma_start(out=out[:, lo:hi], in_=total[:])

@@ -65,16 +65,17 @@ def tile_moe_prv_lin_bias_kernel(tc, uT, wu, w_words, w_scales, b, gate, offs, p
         wu_raw = [[keep.tile([P, 4, WU_LOAD], F32, name=f"wu_raw{a}{c}", align_bytes=64) for c in range(2)] for a in range(PASSES)]
         u_raw = [keep.tile([P, 4, hi - lo], F32, name=f"u_raw{lo}", tag=f"u_raw{lo}", align_bytes=64) for lo, hi in TOKEN_CHUNKS]
 
-        def load_wu(a):
-            for c in range(2):
-                first_column = 512 * a + WU_LOAD * c
-                nc.sync.dma_start(out=wu_raw[a][c][:], in_=wu_rows[:, :, first_column:first_column + WU_LOAD])
+        def load_wu(a, c):
+            first_column = 512 * a + WU_LOAD * c
+            nc.sync.dma_start(out=wu_raw[a][c][:], in_=wu_rows[:, :, first_column:first_column + WU_LOAD])
 
-        load_wu(0)
+        load_wu(0, 0)
+        load_wu(0, 1)
         for i, (lo, hi) in enumerate(TOKEN_CHUNKS):
             nc.sync.dma_start(out=u_raw[i][:], in_=uT_rows[:, :, lo:hi])
+        load_wu(1, 0)
         nc.sync.dma_start(offs_sb[:], offs)
-        load_wu(1)
+        load_wu(1, 1)
         scale_rows = w_scales.rearrange("e a (q r) n -> r q (e a) n", r=4)
         for r in range(4):
             nc.sync.dma_start(

@@ -12,6 +12,7 @@ FP8X4 = mybir.dt.float8_e4m3fn_x4
 MULT = mybir.AluOpType.mult
 ADD = mybir.AluOpType.add
 IDENT = mybir.ActivationFunctionType.Identity
+COPY = mybir.ActivationFunctionType.Copy
 
 K, T, E, C, N, M = 1024, 512, 8, 128, 128, 512
 P = 128
@@ -25,18 +26,18 @@ WU_LOAD = 256
 QUADS = WU_LOAD // 4
 HALF = S // 2
 QUARTER = S // 4
-WINDOWS = (1408, 768)
+WINDOWS = {(0, 0): 1408, (0, 1): 768, (1, 0): 768}
 TOKEN_CHUNKS = ((0, 256), (256, 384), (384, 512))
 TOKEN_HALVES = ((0, 256), (256, 512))
 WU_VECTOR_SHARE = 40
 U_VECTOR_SHARE = 168
 
-FIRST_1 = 0
-SPARE_1 = FIRST_1 + S
-FIRST_0 = SPARE_1 + QUARTER
-ROUNDED_WU = FIRST_0 + S + QUARTER
+FIRST_0 = 0
+SECOND_0 = FIRST_0 + S
+ROUNDED_WU = SECOND_0 + HALF - 128
 STAGE_WORDS = ROUNDED_WU + 1024
-SECOND_1 = (SPARE_1, FIRST_0 + HALF, SPARE_1, FIRST_0 + HALF)
+PIECES_1 = ((0, 256), (256, 512), (512, 1024))
+VECTOR_BIAS = (7,)
 
 
 def tile_moe_prv_lin_bias_kernel(tc, uT, wu, w_words, w_scales, b, gate, offs, pos1, pos2, out):
@@ -55,10 +56,10 @@ def tile_moe_prv_lin_bias_kernel(tc, uT, wu, w_words, w_scales, b, gate, offs, p
 
         w_scale_sb = keep.tile([P, E * PASSES * N], U8, name="w_scale_sb", align_bytes=64)
         nc.vector.memset(w_scale_sb[:].bitcast(I32), 0)
-        pairs = [[keep.tile([P, WINDOWS[h]], U32, name=f"pairs{a}{h}", align_bytes=64) for h in range(2)] for a in range(PASSES)]
-        for a in range(PASSES):
-            for h in range(2):
-                nc.vector.memset(pairs[a][h][:, T:WINDOWS[h]], 0)
+        pairs = {key: keep.tile([P, width], U32, name=f"pairs{key[0]}{key[1]}", align_bytes=64) for key, width in WINDOWS.items()}
+        for key, width in WINDOWS.items():
+            nc.vector.memset(pairs[key][:, T:width], 0)
+        singles = keep.tile([P, 2 * T], BF16, name="singles", align_bytes=64)
 
         wu_rows = wu.rearrange("(p j) c -> p j c", j=4)
         uT_rows = uT.rearrange("(p j) t -> p j t", j=4)
@@ -151,25 +152,41 @@ def tile_moe_prv_lin_bias_kernel(tc, uT, wu, w_words, w_scales, b, gate, offs, p
                     start=True, stop=True,
                 )
             copy(
-                out=pairs[a][h][:, lo:hi].bitcast(BF16).rearrange("p (n e) -> p n e", e=2),
+                out=pairs[(a, h)][:, lo:hi].bitcast(BF16).rearrange("p (n e) -> p n e", e=2),
                 in_=acc.rearrange("p e n -> p n e"),
             )
 
-        def gather(at, a, h, lo, hi):
-            nc.vector.tensor_copy(stage[:, at:at + hi - lo], pairs[a][h][:].indirect(offs_sb[:, lo // 16:hi // 16]))
+        def project_single(e):
+            bank = psum.tile([P, BANK], F32, name="bank")
+            cols = slice(P * e, P * (e + 1))
+            nc.tensor.matmul_mx(
+                out=bank[:],
+                lhsT=wu_codes[(1, 1)][:, cols].bitcast(FP8X4), lhsT_scale=wu_scales[(1, 1)][:, cols],
+                rhs=u_codes[:].bitcast(FP8X4), rhs_scale=u_scales[:],
+                start=True, stop=True,
+            )
+            s_copy(out=singles[:, T * e:T * (e + 1)], in_=bank[:])
 
-        def weave(woven, first, second, copy, lo, hi):
-            step = second - first
-            copy(out=woven[:], in_=stage[:, first:first + 2 * step].rearrange("p (h n) -> p n h", h=2)[:, lo:hi, :])
+        def gather(out, a, h, lo, hi):
+            nc.vector.tensor_copy(out, pairs[(a, h)][:].indirect(offs_sb[:, lo // 16:hi // 16]))
+
+        def gather_singles(out, lo, hi):
+            halves = out.bitcast(BF16).rearrange("p (n e) -> p n e", e=2)
+            for e in range(2):
+                nc.scalar.activation(halves[:, :, e], singles[:, T * e:T * (e + 1)].indirect(offs_sb[:, lo // 16:hi // 16]), COPY)
+
+        def weave(name, both, copy, lo, hi):
+            woven = keep.tile([P, hi - lo, 2], U32, name=name, align_bytes=64)
+            copy(out=woven[:], in_=both.rearrange("p (h n) -> p n h", h=2)[:, lo:hi, :])
+            return woven
 
         x_codes = {}
         x_scales = {}
 
-        def quantize_x(woven, a, lo, hi):
-            codes = keep.tile([P, hi - lo], U32, name=f"x_codes{a}_{lo}", align_bytes=64)
+        def quantize_x(woven, a, lo, hi, codes):
             scales = keep.tile([P, hi - lo], U8, name=f"x_scales{a}_{lo}", align_bytes=64)
             nc.vector.quantize_mx(
-                out=codes[:].bitcast(FP8X4), scales=scales[:],
+                out=codes.bitcast(FP8X4), scales=scales[:],
                 in_=woven[:].rearrange("p n h -> p (n h)").bitcast(BF16),
             )
             for e in range(lo // C, hi // C):
@@ -188,7 +205,10 @@ def tile_moe_prv_lin_bias_kernel(tc, uT, wu, w_words, w_scales, b, gate, offs, p
                     rhs=x_codes[(a, e)].bitcast(FP8X4), rhs_scale=x_scales[(a, e)],
                     start=(a == 0), stop=(a == PASSES - 1),
                 )
-            nc.scalar.activation(out=y_sb[:, e * C:(e + 1) * C], in_=bank[:, 0:C], func=IDENT, bias=b_sb[:, e:e + 1])
+            if e in VECTOR_BIAS:
+                nc.vector.tensor_scalar_add(y_sb[:, e * C:(e + 1) * C], bank[:, 0:C], b_sb[:, e:e + 1])
+            else:
+                nc.scalar.activation(out=y_sb[:, e * C:(e + 1) * C], in_=bank[:, 0:C], func=IDENT, bias=b_sb[:, e:e + 1])
 
         cast_wu(0, 0, v_copy)
         cast_wu(0, 1, v_copy, 0, WU_VECTOR_SHARE)
@@ -207,51 +227,55 @@ def tile_moe_prv_lin_bias_kernel(tc, uT, wu, w_words, w_scales, b, gate, offs, p
         cast_wu(1, 0, g_copy)
         for lo, hi in TOKEN_HALVES:
             project(0, 1, lo, hi, s_copy)
-        for h in range(2):
+        for h in (1, 0):
             cast_wu(1, 1, s_copy, 0, QUADS, 2 * h, 2 * h + 2)
 
-        second_0 = FIRST_0 + S
-        gather(FIRST_0, 0, 0, 0, S)
-        for h in range(2):
+        gather(stage[:, FIRST_0:FIRST_0 + S], 0, 0, 0, S)
+        for h in (1, 0):
             quantize_wu(1, h, f"wu_codes1{h}", 1)
-            gather(second_0 + HALF * h, 0, 1, HALF * h, HALF * (h + 1))
-        woven_0a = keep.tile([P, HALF, 2], U32, name="woven_0a", tag="wu_codes10", align_bytes=64)
+        for e in range(2):
+            project_single(e)
         for lo, hi in TOKEN_HALVES:
             project(1, 0, lo, hi, s_copy)
-        weave(woven_0a, FIRST_0, second_0, s_copy, 0, HALF)
-        for lo, hi in TOKEN_HALVES:
-            project(1, 1, lo, hi, s_copy)
-        gather(FIRST_1, 1, 0, 0, S)
-        woven_0b = keep.tile([P, HALF, 2], U32, name="woven_0b", align_bytes=64)
-        weave(woven_0b, FIRST_0, second_0, s_copy, HALF, S)
+        woven_0 = []
+        for i in range(2):
+            gather(stage[:, SECOND_0 + HALF * i:SECOND_0 + HALF * (i + 1)], 0, 1, HALF * i, HALF * (i + 1))
+            woven_0.append(weave(f"woven_0_{i}", stage[:, FIRST_0:FIRST_0 + 2 * S], nc.gpsimd.tensor_copy, HALF * i, HALF * (i + 1)))
 
-        for i, woven in enumerate((woven_0a, woven_0b)):
-            gather(SECOND_1[i], 1, 1, QUARTER * i, QUARTER * (i + 1))
-            quantize_x(woven, 0, HALF * i, HALF * (i + 1))
-        for i in range(3):
+        both_1 = [keep.tile([P, 2 * (hi - lo)], U32, name=f"both_1_{lo}", tag=f"both_1_{lo}", align_bytes=64) for lo, hi in PIECES_1]
+        for both, (lo, hi) in zip(both_1, PIECES_1):
+            gather(both[:, 0:hi - lo], 1, 0, lo, hi)
+            for q in range(lo, hi, QUARTER):
+                at = hi - lo + q - lo
+                gather_singles(both[:, at:at + QUARTER], q, q + QUARTER)
+        woven_1 = [weave("woven_1_0", both_1[0][:], nc.gpsimd.tensor_copy, 0, QUARTER)]
+        codes_0 = keep.tile([P, S], U32, name="codes_0", tag="both_1_0", align_bytes=64)
+        codes_1 = keep.tile([P, S], U32, name="codes_1", align_bytes=64)
+
+        def finish(i):
             lo, hi = QUARTER * i, QUARTER * (i + 1)
-            woven = keep.tile([P, QUARTER, 2], U32, name=f"woven_1_{i}", align_bytes=64)
-            weave(woven, FIRST_1 + lo, SECOND_1[i], s_copy, 0, QUARTER)
-            if i < 2:
-                gather(SECOND_1[i + 2], 1, 1, lo + HALF, hi + HALF)
-            else:
-                last = [keep.tile([P, C, 2], U32, name=f"woven_last{j}", align_bytes=64) for j in range(2)]
-                for j, copy in enumerate((v_copy, s_copy)):
-                    weave(last[j], FIRST_1 + hi, SECOND_1[3], copy, C * j, C * (j + 1))
-            quantize_x(woven, 1, lo, hi)
+            quantize_x(woven_1[i], 1, lo, hi, codes_1[:, lo:hi])
             for e in range(lo // C, hi // C):
                 expert(e)
-        for j in range(2):
-            quantize_x(last[j], 1, S - QUARTER + C * j, S - QUARTER + C * (j + 1))
-        for e in range(E - 2, E):
-            expert(e)
+
+        for i in range(2):
+            quantize_x(woven_0[i], 0, HALF * i, HALF * (i + 1), codes_0[:, HALF * i:HALF * (i + 1)])
+        woven_1.append(weave("woven_1_1", both_1[1][:], v_copy, 0, QUARTER))
+        finish(0)
+        woven_1.append(weave("woven_1_2", both_1[2][:], v_copy, 0, QUARTER))
+        finish(1)
+        woven_1.append(weave("woven_1_3", both_1[2][:], v_copy, QUARTER, HALF))
+        finish(2)
+        finish(3)
 
         first = keep.tile([P, T], F32, name="first")
         nc.vector.tensor_tensor(first[:], y_sb[:].indirect(pos1_sb[:]), gate_sb[0][:], MULT)
         second = [keep.tile([P, hi - lo], F32, name=f"second{lo}") for lo, hi in TOKEN_HALVES]
+        gated = [keep.tile([P, hi - lo], F32, name=f"gated{lo}") for lo, hi in TOKEN_HALVES]
         for i, (lo, hi) in enumerate(TOKEN_HALVES):
-            nc.vector.tensor_tensor(second[i][:], y_sb[:].indirect(pos2_sb[:, lo // 16:hi // 16]), gate_sb[1][:, lo:hi], MULT)
+            nc.scalar.activation(second[i][:], y_sb[:].indirect(pos2_sb[:, lo // 16:hi // 16]), COPY)
+            nc.vector.tensor_tensor(gated[i][:], second[i][:], gate_sb[1][:, lo:hi], MULT)
         for i, (lo, hi) in enumerate(TOKEN_HALVES):
             total = keep.tile([P, hi - lo], F32, name=f"total{lo}")
-            nc.vector.tensor_tensor(total[:], first[:, lo:hi], second[i][:], ADD)
+            nc.vector.tensor_tensor(total[:], first[:, lo:hi], gated[i][:], ADD)
             (nc.sync, nc.scalar)[i].dma_start(out=out[:, lo:hi], in_=total[:])

@@ -26,7 +26,7 @@ WU_LOAD = 256
 QUADS = WU_LOAD // 4
 HALF = S // 2
 QUARTER = S // 4
-WINDOWS = {(0, 0): 1408, (0, 1): 768, (1, 0): 768}
+WINDOWS = {(0, 0): 1024, (0, 1): 768, (1, 1): 768}
 TOKEN_CHUNKS = ((0, 256), (256, 384), (384, 512))
 TOKEN_HALVES = ((0, 256), (256, 512))
 WU_VECTOR_SHARE = 40
@@ -34,10 +34,10 @@ U_VECTOR_SHARE = 168
 
 FIRST_0 = 0
 SECOND_0 = FIRST_0 + S
-ROUNDED_WU = SECOND_0 + HALF - 128
-STAGE_WORDS = ROUNDED_WU + 1024
-PIECES_1 = ((0, 256), (256, 512), (512, 1024))
-VECTOR_BIAS = (7,)
+STAGE_WORDS = SECOND_0 + S
+LAST_WU = SECOND_0 - QUARTER
+WOVEN = ((1, 0), (0, 0), (0, 1), (0, 2), (0, 3), (1, 1), (1, 2), (1, 3))
+VECTOR_BIAS = (5, 7)
 
 
 def tile_moe_prv_lin_bias_kernel(tc, uT, wu, w_words, w_scales, b, gate, offs, pos1, pos2, out):
@@ -63,12 +63,14 @@ def tile_moe_prv_lin_bias_kernel(tc, uT, wu, w_words, w_scales, b, gate, offs, p
 
         wu_rows = wu.rearrange("(p j) c -> p j c", j=4)
         uT_rows = uT.rearrange("(p j) t -> p j t", j=4)
-        wu_raw = [[keep.tile([P, 4, WU_LOAD], F32, name=f"wu_raw{a}{c}", align_bytes=64) for c in range(2)] for a in range(PASSES)]
+        stage = keep.tile([P, STAGE_WORDS], U32, name="stage", align_bytes=64)
+        wu_raw = {key: keep.tile([P, 4, WU_LOAD], F32, name=f"wu_raw{key[0]}{key[1]}", align_bytes=64)[:] for key in ((0, 0), (0, 1), (1, 0))}
+        wu_raw[(1, 1)] = stage[:, LAST_WU:LAST_WU + 4 * WU_LOAD].bitcast(F32).rearrange("p (j c) -> p j c", j=4)
         u_raw = [keep.tile([P, 4, hi - lo], F32, name=f"u_raw{lo}", tag=f"u_raw{lo}", align_bytes=64) for lo, hi in TOKEN_CHUNKS]
 
         def load_wu(a, c):
             first_column = 512 * a + WU_LOAD * c
-            nc.sync.dma_start(out=wu_raw[a][c][:], in_=wu_rows[:, :, first_column:first_column + WU_LOAD])
+            nc.sync.dma_start(out=wu_raw[(a, c)], in_=wu_rows[:, :, first_column:first_column + WU_LOAD])
 
         load_wu(0, 0)
         load_wu(0, 1)
@@ -96,8 +98,7 @@ def tile_moe_prv_lin_bias_kernel(tc, uT, wu, w_words, w_scales, b, gate, offs, p
         nc.sync.dma_start(pos1_sb[:], pos1)
         nc.sync.dma_start(pos2_sb[:], pos2)
 
-        stage = keep.tile([P, STAGE_WORDS], U32, name="stage", align_bytes=64)
-        wu_bf = stage[:, ROUNDED_WU:STAGE_WORDS].bitcast(BF16).rearrange("p (t m j) -> p t m j", t=4, j=4)
+        wu_bf = keep.tile([P, 4, P, 4], BF16, name="wu_bf", align_bytes=64)
         wu_codes = {}
         wu_scales = {}
         u_bf = [keep.tile([P, hi - lo, 4], BF16, name=f"u_bf{lo}", align_bytes=64) for lo, hi in TOKEN_CHUNKS]
@@ -112,7 +113,7 @@ def tile_moe_prv_lin_bias_kernel(tc, uT, wu, w_words, w_scales, b, gate, offs, p
         def cast_wu(a, c, copy, lo=0, hi=QUADS, t0=0, t1=4):
             copy(
                 out=wu_bf[:, t0:t1, QUADS * c + lo:QUADS * c + hi, :].rearrange("p t m j -> p m j t"),
-                in_=wu_raw[a][c][:, :, 4 * lo:4 * hi].rearrange("p j (m t) -> p m j t", t=4)[:, :, :, t0:t1],
+                in_=wu_raw[(a, c)][:, :, 4 * lo:4 * hi].rearrange("p j (m t) -> p m j t", t=4)[:, :, :, t0:t1],
             )
 
         def quantize_wu(a, h, tag, outputs_a_call):
@@ -156,42 +157,48 @@ def tile_moe_prv_lin_bias_kernel(tc, uT, wu, w_words, w_scales, b, gate, offs, p
                 in_=acc.rearrange("p e n -> p n e"),
             )
 
-        def project_single(e):
+        def project_single(e, lo, hi):
             bank = psum.tile([P, BANK], F32, name="bank")
             cols = slice(P * e, P * (e + 1))
             nc.tensor.matmul_mx(
-                out=bank[:],
-                lhsT=wu_codes[(1, 1)][:, cols].bitcast(FP8X4), lhsT_scale=wu_scales[(1, 1)][:, cols],
-                rhs=u_codes[:].bitcast(FP8X4), rhs_scale=u_scales[:],
+                out=bank[:, 0:hi - lo],
+                lhsT=wu_codes[(1, 0)][:, cols].bitcast(FP8X4), lhsT_scale=wu_scales[(1, 0)][:, cols],
+                rhs=u_codes[:, lo:hi].bitcast(FP8X4), rhs_scale=u_scales[:, lo:hi],
                 start=True, stop=True,
             )
-            s_copy(out=singles[:, T * e:T * (e + 1)], in_=bank[:])
+            s_copy(out=singles[:, T * e + lo:T * e + hi], in_=bank[:, 0:hi - lo])
 
         def gather(out, a, h, lo, hi):
             nc.vector.tensor_copy(out, pairs[(a, h)][:].indirect(offs_sb[:, lo // 16:hi // 16]))
 
-        def gather_singles(out, lo, hi):
+        def gather_single(out, e, lo, hi):
             halves = out.bitcast(BF16).rearrange("p (n e) -> p n e", e=2)
-            for e in range(2):
-                nc.scalar.activation(halves[:, :, e], singles[:, T * e:T * (e + 1)].indirect(offs_sb[:, lo // 16:hi // 16]), COPY)
+            nc.scalar.activation(halves[:, :, e], singles[:, T * e:T * (e + 1)].indirect(offs_sb[:, lo // 16:hi // 16]), COPY)
 
-        def weave(name, both, copy, lo, hi):
-            woven = keep.tile([P, hi - lo, 2], U32, name=name, align_bytes=64)
-            copy(out=woven[:], in_=both.rearrange("p (h n) -> p n h", h=2)[:, lo:hi, :])
-            return woven
+        woven = keep.tile([P, 4 * S], U32, name="woven", align_bytes=64)
+
+        def weave(a, q, count, both, lo, copy):
+            at = HALF * WOVEN.index((a, q))
+            copy(
+                out=woven[:, at:at + HALF * count].rearrange("p (n h) -> p n h", h=2),
+                in_=both.rearrange("p (h n) -> p n h", h=2)[:, lo:lo + QUARTER * count, :],
+            )
 
         x_codes = {}
         x_scales = {}
 
-        def quantize_x(woven, a, lo, hi, codes):
-            scales = keep.tile([P, hi - lo], U8, name=f"x_scales{a}_{lo}", align_bytes=64)
+        def quantize_x(first, count, tag):
+            codes = keep.tile([P, C * count], U32, name=f"x_codes{first}", tag=tag, align_bytes=64)
+            scales = keep.tile([P, C * count], U8, name=f"x_scales{first}", align_bytes=64)
             nc.vector.quantize_mx(
-                out=codes.bitcast(FP8X4), scales=scales[:],
-                in_=woven[:].rearrange("p n h -> p (n h)").bitcast(BF16),
+                out=codes[:].bitcast(FP8X4), scales=scales[:],
+                in_=woven[:, 2 * C * first:2 * C * (first + count)].bitcast(BF16),
             )
-            for e in range(lo // C, hi // C):
-                x_codes[(a, e)] = codes[:, e * C - lo:(e + 1) * C - lo]
-                x_scales[(a, e)] = scales[:, e * C - lo:(e + 1) * C - lo]
+            for i in range(count):
+                a, q = WOVEN[(first + i) // 2]
+                e = 2 * q + (first + i) % 2
+                x_codes[(a, e)] = codes[:, C * i:C * (i + 1)]
+                x_scales[(a, e)] = scales[:, C * i:C * (i + 1)]
 
         y_sb = keep.tile([P, S], F32, name="y_sb")
 
@@ -225,48 +232,42 @@ def tile_moe_prv_lin_bias_kernel(tc, uT, wu, w_words, w_scales, b, gate, offs, p
         for (lo, hi), copy in zip(TOKEN_CHUNKS, (s_copy, v_copy, s_copy)):
             project(0, 0, lo, hi, copy)
         cast_wu(1, 0, g_copy)
-        for lo, hi in TOKEN_HALVES:
-            project(0, 1, lo, hi, s_copy)
-        for h in (1, 0):
-            cast_wu(1, 1, s_copy, 0, QUADS, 2 * h, 2 * h + 2)
+        cast_wu(1, 1, g_copy, 0, QUADS // 2)
+        project(0, 1, *TOKEN_HALVES[0], s_copy)
+        cast_wu(1, 1, s_copy, QUADS // 2, QUADS)
+        project(0, 1, *TOKEN_HALVES[1], s_copy)
 
-        gather(stage[:, FIRST_0:FIRST_0 + S], 0, 0, 0, S)
-        for h in (1, 0):
-            quantize_wu(1, h, f"wu_codes1{h}", 1)
+        for h, (lo, hi) in enumerate(((0, S - QUARTER), (S - QUARTER, S))):
+            gather(stage[:, FIRST_0 + lo:FIRST_0 + hi], 0, 0, lo, hi)
+            quantize_wu(1, h, f"wu_codes1{h}", 2)
+        both_1 = [keep.tile([P, S], U32, name=f"both_1_{i}", tag=f"both_1_{i}", align_bytes=64) for i in range(2)]
         for e in range(2):
-            project_single(e)
+            for lo, hi in TOKEN_HALVES:
+                project_single(e, lo, hi)
         for lo, hi in TOKEN_HALVES:
-            project(1, 0, lo, hi, s_copy)
-        woven_0 = []
+            project(1, 1, lo, hi, s_copy)
         for i in range(2):
             gather(stage[:, SECOND_0 + HALF * i:SECOND_0 + HALF * (i + 1)], 0, 1, HALF * i, HALF * (i + 1))
-            woven_0.append(weave(f"woven_0_{i}", stage[:, FIRST_0:FIRST_0 + 2 * S], nc.gpsimd.tensor_copy, HALF * i, HALF * (i + 1)))
-
-        both_1 = [keep.tile([P, 2 * (hi - lo)], U32, name=f"both_1_{lo}", tag=f"both_1_{lo}", align_bytes=64) for lo, hi in PIECES_1]
-        for both, (lo, hi) in zip(both_1, PIECES_1):
-            gather(both[:, 0:hi - lo], 1, 0, lo, hi)
-            for q in range(lo, hi, QUARTER):
-                at = hi - lo + q - lo
-                gather_singles(both[:, at:at + QUARTER], q, q + QUARTER)
-        woven_1 = [weave("woven_1_0", both_1[0][:], nc.gpsimd.tensor_copy, 0, QUARTER)]
-        codes_0 = keep.tile([P, S], U32, name="codes_0", tag="both_1_0", align_bytes=64)
-        codes_1 = keep.tile([P, S], U32, name="codes_1", align_bytes=64)
-
-        def finish(i):
-            lo, hi = QUARTER * i, QUARTER * (i + 1)
-            quantize_x(woven_1[i], 1, lo, hi, codes_1[:, lo:hi])
-            for e in range(lo // C, hi // C):
-                expert(e)
+            weave(0, 2 * i, 2, stage[:], HALF * i, nc.gpsimd.tensor_copy)
 
         for i in range(2):
-            quantize_x(woven_0[i], 0, HALF * i, HALF * (i + 1), codes_0[:, HALF * i:HALF * (i + 1)])
-        woven_1.append(weave("woven_1_1", both_1[1][:], v_copy, 0, QUARTER))
-        finish(0)
-        woven_1.append(weave("woven_1_2", both_1[2][:], v_copy, 0, QUARTER))
-        finish(1)
-        woven_1.append(weave("woven_1_3", both_1[2][:], v_copy, QUARTER, HALF))
-        finish(2)
-        finish(3)
+            gather(both_1[i][:, HALF:S], 1, 1, HALF * i, HALF * (i + 1))
+        for q in range(4):
+            at = QUARTER * (q % 2)
+            for e in range(2):
+                gather_single(both_1[q // 2][:, at:at + QUARTER], e, QUARTER * q, QUARTER * (q + 1))
+        weave(1, 0, 1, both_1[0][:], 0, nc.gpsimd.tensor_copy)
+        weave(1, 1, 1, both_1[0][:], QUARTER, v_copy)
+        quantize_x(0, 4, "x_codes0")
+        expert(0)
+        expert(1)
+        quantize_x(4, 4, "both_1_0")
+        weave(1, 2, 1, both_1[1][:], 0, v_copy)
+        weave(1, 3, 1, both_1[1][:], QUARTER, s_copy)
+        for first, count, experts in ((8, 4, (2, 3)), (12, 2, (4, 5)), (14, 1, (6,)), (15, 1, (7,))):
+            quantize_x(first, count, f"x_codes{first}")
+            for e in experts:
+                expert(e)
 
         first = keep.tile([P, T], F32, name="first")
         nc.vector.tensor_tensor(first[:], y_sb[:].indirect(pos1_sb[:]), gate_sb[0][:], MULT)

@@ -37,7 +37,8 @@ SECOND_0 = FIRST_0 + S
 STAGE_WORDS = SECOND_0 + S
 LAST_WU = SECOND_0 - QUARTER
 WOVEN = ((1, 0), (0, 0), (0, 1), (0, 2), (0, 3), (1, 1), (1, 2), (1, 3))
-VECTOR_BIAS = (5, 7)
+SCALAR_PIECES = ((0, 256), (256, 512), (512, 768), (768, 896), (896, 1024))
+VECTOR_BIAS = (4, 7)
 
 
 def tile_moe_prv_lin_bias_kernel(tc, uT, wu, w_words, w_scales, b, gate, offs, pos1, pos2, out):
@@ -63,7 +64,7 @@ def tile_moe_prv_lin_bias_kernel(tc, uT, wu, w_words, w_scales, b, gate, offs, p
 
         wu_rows = wu.rearrange("(p j) c -> p j c", j=4)
         uT_rows = uT.rearrange("(p j) t -> p j t", j=4)
-        stage = keep.tile([P, STAGE_WORDS], U32, name="stage", align_bytes=64)
+        stage = keep.tile([P, STAGE_WORDS], U32, name="stage", tag="stage", align_bytes=64)
         wu_raw = {key: keep.tile([P, 4, WU_LOAD], F32, name=f"wu_raw{key[0]}{key[1]}", align_bytes=64)[:] for key in ((0, 0), (0, 1), (1, 0))}
         wu_raw[(1, 1)] = stage[:, LAST_WU:LAST_WU + 4 * WU_LOAD].bitcast(F32).rearrange("p (j c) -> p j c", j=4)
         u_raw = [keep.tile([P, 4, hi - lo], F32, name=f"u_raw{lo}", tag=f"u_raw{lo}", align_bytes=64) for lo, hi in TOKEN_CHUNKS]
@@ -177,11 +178,11 @@ def tile_moe_prv_lin_bias_kernel(tc, uT, wu, w_words, w_scales, b, gate, offs, p
 
         woven = keep.tile([P, 4 * S], U32, name="woven", align_bytes=64)
 
-        def weave(a, q, count, both, lo, copy):
-            at = HALF * WOVEN.index((a, q))
+        def weave(a, lo, hi, both, first, copy):
+            at = HALF * WOVEN.index((a, lo // QUARTER)) + 2 * (lo % QUARTER)
             copy(
-                out=woven[:, at:at + HALF * count].rearrange("p (n h) -> p n h", h=2),
-                in_=both.rearrange("p (h n) -> p n h", h=2)[:, lo:lo + QUARTER * count, :],
+                out=woven[:, at:at + 2 * (hi - lo)].rearrange("p (n h) -> p n h", h=2),
+                in_=both.rearrange("p (h n) -> p n h", h=2)[:, first:first + hi - lo, :],
             )
 
         x_codes = {}
@@ -202,16 +203,28 @@ def tile_moe_prv_lin_bias_kernel(tc, uT, wu, w_words, w_scales, b, gate, offs, p
 
         y_sb = keep.tile([P, S], F32, name="y_sb")
 
+        banks = {}
+
+        def expert_pass(e, a):
+            if a == 0:
+                banks[e] = psum.tile([P, BANK], F32, name="bank")
+            g = e * PASSES + a
+            nc.tensor.matmul_mx(
+                out=banks[e][:, 0:C],
+                lhsT=w_codes[g // per_load][:, g % per_load, :].bitcast(FP8X4), lhsT_scale=w_scale_sb[:, g * N:(g + 1) * N],
+                rhs=x_codes[(a, e)].bitcast(FP8X4), rhs_scale=x_scales[(a, e)],
+                start=(a == 0), stop=(a == PASSES - 1),
+            )
+
         def expert(e):
-            bank = psum.tile([P, BANK], F32, name="bank")
-            for a in range(PASSES):
-                g = e * PASSES + a
-                nc.tensor.matmul_mx(
-                    out=bank[:, 0:C],
-                    lhsT=w_codes[g // per_load][:, g % per_load, :].bitcast(FP8X4), lhsT_scale=w_scale_sb[:, g * N:(g + 1) * N],
-                    rhs=x_codes[(a, e)].bitcast(FP8X4), rhs_scale=x_scales[(a, e)],
-                    start=(a == 0), stop=(a == PASSES - 1),
-                )
+            if e not in banks:
+                expert_pass(e, 0)
+            expert_pass(e, 1)
+            if e not in VECTOR_BIAS:
+                add_bias(e)
+
+        def add_bias(e):
+            bank = banks[e]
             if e in VECTOR_BIAS:
                 nc.vector.tensor_scalar_add(y_sb[:, e * C:(e + 1) * C], bank[:, 0:C], b_sb[:, e:e + 1])
             else:
@@ -248,26 +261,30 @@ def tile_moe_prv_lin_bias_kernel(tc, uT, wu, w_words, w_scales, b, gate, offs, p
             project(1, 1, lo, hi, s_copy)
         for i in range(2):
             gather(stage[:, SECOND_0 + HALF * i:SECOND_0 + HALF * (i + 1)], 0, 1, HALF * i, HALF * (i + 1))
-            weave(0, 2 * i, 2, stage[:], HALF * i, nc.gpsimd.tensor_copy)
+            weave(0, HALF * i, HALF * (i + 1), stage[:], HALF * i, nc.gpsimd.tensor_copy)
 
         for i in range(2):
             gather(both_1[i][:, HALF:S], 1, 1, HALF * i, HALF * (i + 1))
-        for q in range(4):
-            at = QUARTER * (q % 2)
+        for lo, hi in SCALAR_PIECES:
             for e in range(2):
-                gather_single(both_1[q // 2][:, at:at + QUARTER], e, QUARTER * q, QUARTER * (q + 1))
-        weave(1, 0, 1, both_1[0][:], 0, nc.gpsimd.tensor_copy)
-        weave(1, 1, 1, both_1[0][:], QUARTER, v_copy)
+                gather_single(both_1[lo // HALF][:, lo % HALF:lo % HALF + hi - lo], e, lo, hi)
+        weave(1, 0, 256, both_1[0][:], 0, nc.gpsimd.tensor_copy)
+        quantize_x(4, 4, "stage")
+        for e in (2, 3):
+            expert_pass(e, 0)
+        weave(1, 256, 512, both_1[0][:], 256, v_copy)
         quantize_x(0, 4, "x_codes0")
         expert(0)
         expert(1)
-        quantize_x(4, 4, "both_1_0")
-        weave(1, 2, 1, both_1[1][:], 0, v_copy)
-        weave(1, 3, 1, both_1[1][:], QUARTER, s_copy)
-        for first, count, experts in ((8, 4, (2, 3)), (12, 2, (4, 5)), (14, 1, (6,)), (15, 1, (7,))):
+        for lo, hi, first, count, experts in ((512, 768, 8, 4, (2, 3)), (768, 896, 12, 2, (4, 5)), (896, 1024, 14, 1, (6,))):
+            weave(1, lo, hi, both_1[1][:], lo - HALF, v_copy)
             quantize_x(first, count, f"x_codes{first}")
             for e in experts:
                 expert(e)
+        quantize_x(15, 1, "x_codes15")
+        expert(7)
+        for e in VECTOR_BIAS:
+            add_bias(e)
 
         first = keep.tile([P, T], F32, name="first")
         nc.vector.tensor_tensor(first[:], y_sb[:].indirect(pos1_sb[:]), gate_sb[0][:], MULT)

@@ -26,7 +26,7 @@ WU_LOAD = 256
 QUADS = WU_LOAD // 4
 HALF = S // 2
 QUARTER = S // 4
-WINDOWS = {(0, 0): 1024, (0, 1): 768, (1, 1): 768}
+WINDOWS = {(0, 0): 1024, (0, 1): 768, (1, 0): 768}
 TOKEN_CHUNKS = ((0, 256), (256, 384), (384, 512))
 TOKEN_HALVES = ((0, 256), (256, 512))
 WU_VECTOR_SHARE = 40
@@ -163,7 +163,7 @@ def tile_moe_prv_lin_bias_kernel(tc, uT, wu, w_words, w_scales, b, gate, offs, p
             cols = slice(P * e, P * (e + 1))
             nc.tensor.matmul_mx(
                 out=bank[:, 0:hi - lo],
-                lhsT=wu_codes[(1, 0)][:, cols].bitcast(FP8X4), lhsT_scale=wu_scales[(1, 0)][:, cols],
+                lhsT=wu_codes[(1, 1)][:, cols].bitcast(FP8X4), lhsT_scale=wu_scales[(1, 1)][:, cols],
                 rhs=u_codes[:, lo:hi].bitcast(FP8X4), rhs_scale=u_scales[:, lo:hi],
                 start=True, stop=True,
             )
@@ -254,20 +254,19 @@ def tile_moe_prv_lin_bias_kernel(tc, uT, wu, w_words, w_scales, b, gate, offs, p
             gather(stage[:, FIRST_0 + lo:FIRST_0 + hi], 0, 0, lo, hi)
             quantize_wu(1, h, f"wu_codes1{h}", 2)
         both_1 = [keep.tile([P, S], U32, name=f"both_1_{i}", tag=f"both_1_{i}", align_bytes=64) for i in range(2)]
-        for e in range(2):
-            for lo, hi in TOKEN_HALVES:
-                project_single(e, lo, hi)
         for lo, hi in TOKEN_HALVES:
-            project(1, 1, lo, hi, s_copy)
+            project(1, 0, lo, hi, s_copy)
+        for e in range(2):
+            project_single(e, 0, T)
         for i in range(2):
             gather(stage[:, SECOND_0 + HALF * i:SECOND_0 + HALF * (i + 1)], 0, 1, HALF * i, HALF * (i + 1))
             weave(0, HALF * i, HALF * (i + 1), stage[:], HALF * i, nc.gpsimd.tensor_copy)
 
         for i in range(2):
-            gather(both_1[i][:, HALF:S], 1, 1, HALF * i, HALF * (i + 1))
+            gather(both_1[i][:, 0:HALF], 1, 0, HALF * i, HALF * (i + 1))
         for lo, hi in SCALAR_PIECES:
             for e in range(2):
-                gather_single(both_1[lo // HALF][:, lo % HALF:lo % HALF + hi - lo], e, lo, hi)
+                gather_single(both_1[lo // HALF][:, HALF + lo % HALF:HALF + lo % HALF + hi - lo], e, lo, hi)
         weave(1, 0, 256, both_1[0][:], 0, nc.gpsimd.tensor_copy)
         quantize_x(4, 4, "stage")
         for e in (2, 3):

@@ -31,11 +31,12 @@ TOKEN_CHUNKS = ((0, 256), (256, 384), (384, 512))
 TOKEN_HALVES = ((0, 256), (256, 512))
 WU_VECTOR_SHARE = 40
 U_VECTOR_SHARE = 168
+FIRST_CUT = S - QUARTER
 
 FIRST_0 = 0
 SECOND_0 = FIRST_0 + S
 STAGE_WORDS = SECOND_0 + S
-LAST_WU = SECOND_0 - QUARTER
+LAST_WU = FIRST_0 + FIRST_CUT
 WOVEN = ((1, 0), (0, 0), (0, 1), (0, 2), (0, 3), (1, 1), (1, 2), (1, 3))
 SCALAR_PIECES = ((0, 256), (256, 512), (512, 768), (768, 896), (896, 1024))
 VECTOR_BIAS = (4, 7)
@@ -111,22 +112,20 @@ def tile_moe_prv_lin_bias_kernel(tc, uT, wu, w_words, w_scales, b, gate, offs, p
         def g_copy(out, in_):
             nc.gpsimd.tensor_scalar(out.rearrange("p m j t -> p m t j"), in_.rearrange("p m j t -> p m t j"), 1.0, 0.0, MULT, ADD)
 
-        def cast_wu(a, c, copy, lo=0, hi=QUADS, t0=0, t1=4):
+        def cast_wu(a, c, copy, lo=0, hi=QUADS):
             copy(
-                out=wu_bf[:, t0:t1, QUADS * c + lo:QUADS * c + hi, :].rearrange("p t m j -> p m j t"),
-                in_=wu_raw[(a, c)][:, :, 4 * lo:4 * hi].rearrange("p j (m t) -> p m j t", t=4)[:, :, :, t0:t1],
+                out=wu_bf[:, :, QUADS * c + lo:QUADS * c + hi, :].rearrange("p t m j -> p m j t"),
+                in_=wu_raw[(a, c)][:, :, 4 * lo:4 * hi].rearrange("p j (m t) -> p m j t", t=4),
             )
 
-        def quantize_wu(a, h, tag, outputs_a_call):
+        def quantize_wu(a, h, tag):
             wu_codes[(a, h)] = keep.tile([P, 2 * P], U32, name=f"wu_codes{a}{h}", tag=tag, align_bytes=64)
             wu_scales[(a, h)] = keep.tile([P, 2 * P], U8, name=f"wu_scales{a}{h}", align_bytes=64)
-            for e0 in range(0, 2, outputs_a_call):
-                e1 = e0 + outputs_a_call
-                nc.vector.quantize_mx(
-                    out=wu_codes[(a, h)][:, P * e0:P * e1].bitcast(FP8X4),
-                    scales=wu_scales[(a, h)][:, P * e0:P * e1],
-                    in_=wu_bf[:, 2 * h + e0:2 * h + e1, :, :].rearrange("p t m j -> p (t m j)"),
-                )
+            nc.vector.quantize_mx(
+                out=wu_codes[(a, h)][:].bitcast(FP8X4),
+                scales=wu_scales[(a, h)][:],
+                in_=wu_bf[:, 2 * h:2 * h + 2, :, :].rearrange("p t m j -> p (t m j)"),
+            )
 
         def cast_u(i, copy, lo=0, hi=128):
             copy(
@@ -158,16 +157,16 @@ def tile_moe_prv_lin_bias_kernel(tc, uT, wu, w_words, w_scales, b, gate, offs, p
                 in_=acc.rearrange("p e n -> p n e"),
             )
 
-        def project_single(e, lo, hi):
+        def project_single(e):
             bank = psum.tile([P, BANK], F32, name="bank")
             cols = slice(P * e, P * (e + 1))
             nc.tensor.matmul_mx(
-                out=bank[:, 0:hi - lo],
+                out=bank[:],
                 lhsT=wu_codes[(1, 1)][:, cols].bitcast(FP8X4), lhsT_scale=wu_scales[(1, 1)][:, cols],
-                rhs=u_codes[:, lo:hi].bitcast(FP8X4), rhs_scale=u_scales[:, lo:hi],
+                rhs=u_codes[:].bitcast(FP8X4), rhs_scale=u_scales[:],
                 start=True, stop=True,
             )
-            s_copy(out=singles[:, T * e + lo:T * e + hi], in_=bank[:, 0:hi - lo])
+            s_copy(out=singles[:, T * e:T * (e + 1)], in_=bank[:])
 
         def gather(out, a, h, lo, hi):
             nc.vector.tensor_copy(out, pairs[(a, h)][:].indirect(offs_sb[:, lo // 16:hi // 16]))
@@ -178,28 +177,32 @@ def tile_moe_prv_lin_bias_kernel(tc, uT, wu, w_words, w_scales, b, gate, offs, p
 
         woven = keep.tile([P, 4 * S], U32, name="woven", align_bytes=64)
 
-        def weave(a, lo, hi, both, first, copy):
-            at = HALF * WOVEN.index((a, lo // QUARTER)) + 2 * (lo % QUARTER)
+        def woven_at(a, slot):
+            return HALF * WOVEN.index((a, slot // QUARTER)) + 2 * (slot % QUARTER)
+
+        def weave(a, lo, hi, both, column, copy):
+            at = woven_at(a, lo)
             copy(
                 out=woven[:, at:at + 2 * (hi - lo)].rearrange("p (n h) -> p n h", h=2),
-                in_=both.rearrange("p (h n) -> p n h", h=2)[:, first:first + hi - lo, :],
+                in_=both.rearrange("p (h n) -> p n h", h=2)[:, column:column + hi - lo, :],
             )
 
         x_codes = {}
         x_scales = {}
 
-        def quantize_x(first, count, tag):
-            codes = keep.tile([P, C * count], U32, name=f"x_codes{first}", tag=tag, align_bytes=64)
-            scales = keep.tile([P, C * count], U8, name=f"x_scales{first}", align_bytes=64)
+        def quantize_x(parts, tag=None):
+            a0, e0 = parts[0]
+            at = woven_at(a0, C * e0)
+            name = f"x_codes{a0}{e0}"
+            codes = keep.tile([P, C * len(parts)], U32, name=name, tag=tag or name, align_bytes=64)
+            scales = keep.tile([P, C * len(parts)], U8, name=f"x_scales{a0}{e0}", align_bytes=64)
             nc.vector.quantize_mx(
                 out=codes[:].bitcast(FP8X4), scales=scales[:],
-                in_=woven[:, 2 * C * first:2 * C * (first + count)].bitcast(BF16),
+                in_=woven[:, at:at + 2 * C * len(parts)].bitcast(BF16),
             )
-            for i in range(count):
-                a, q = WOVEN[(first + i) // 2]
-                e = 2 * q + (first + i) % 2
-                x_codes[(a, e)] = codes[:, C * i:C * (i + 1)]
-                x_scales[(a, e)] = scales[:, C * i:C * (i + 1)]
+            for i, part in enumerate(parts):
+                x_codes[part] = codes[:, C * i:C * (i + 1)]
+                x_scales[part] = scales[:, C * i:C * (i + 1)]
 
         y_sb = keep.tile([P, S], F32, name="y_sb")
 
@@ -216,24 +219,15 @@ def tile_moe_prv_lin_bias_kernel(tc, uT, wu, w_words, w_scales, b, gate, offs, p
                 start=(a == 0), stop=(a == PASSES - 1),
             )
 
-        def expert(e):
-            if e not in banks:
-                expert_pass(e, 0)
+        def finish_expert(e):
             expert_pass(e, 1)
             if e not in VECTOR_BIAS:
-                add_bias(e)
-
-        def add_bias(e):
-            bank = banks[e]
-            if e in VECTOR_BIAS:
-                nc.vector.tensor_scalar_add(y_sb[:, e * C:(e + 1) * C], bank[:, 0:C], b_sb[:, e:e + 1])
-            else:
-                nc.scalar.activation(out=y_sb[:, e * C:(e + 1) * C], in_=bank[:, 0:C], func=IDENT, bias=b_sb[:, e:e + 1])
+                nc.scalar.activation(out=y_sb[:, e * C:(e + 1) * C], in_=banks[e][:, 0:C], func=IDENT, bias=b_sb[:, e:e + 1])
 
         cast_wu(0, 0, v_copy)
         cast_wu(0, 1, v_copy, 0, WU_VECTOR_SHARE)
         cast_wu(0, 1, s_copy, WU_VECTOR_SHARE, QUADS)
-        quantize_wu(0, 0, "wu_codes00", 2)
+        quantize_wu(0, 0, "wu_codes00")
         cast_u(0, v_copy, 0, U_VECTOR_SHARE)
         cast_u(0, s_copy, U_VECTOR_SHARE, TOKEN_CHUNKS[0][1])
         quantize_u(0)
@@ -241,7 +235,7 @@ def tile_moe_prv_lin_bias_kernel(tc, uT, wu, w_words, w_scales, b, gate, offs, p
         cast_u(2, v_copy)
         quantize_u(1)
         quantize_u(2)
-        quantize_wu(0, 1, f"u_raw{TOKEN_CHUNKS[2][0]}", 2)
+        quantize_wu(0, 1, f"u_raw{TOKEN_CHUNKS[2][0]}")
         for (lo, hi), copy in zip(TOKEN_CHUNKS, (s_copy, v_copy, s_copy)):
             project(0, 0, lo, hi, copy)
         cast_wu(1, 0, g_copy)
@@ -250,14 +244,14 @@ def tile_moe_prv_lin_bias_kernel(tc, uT, wu, w_words, w_scales, b, gate, offs, p
         cast_wu(1, 1, s_copy, QUADS // 2, QUADS)
         project(0, 1, *TOKEN_HALVES[1], s_copy)
 
-        for h, (lo, hi) in enumerate(((0, S - QUARTER), (S - QUARTER, S))):
+        for h, (lo, hi) in enumerate(((0, FIRST_CUT), (FIRST_CUT, S))):
             gather(stage[:, FIRST_0 + lo:FIRST_0 + hi], 0, 0, lo, hi)
-            quantize_wu(1, h, f"wu_codes1{h}", 2)
-        both_1 = [keep.tile([P, S], U32, name=f"both_1_{i}", tag=f"both_1_{i}", align_bytes=64) for i in range(2)]
+            quantize_wu(1, h, f"wu_codes1{h}")
+        both_1 = [keep.tile([P, S], U32, name=f"both_1_{i}", align_bytes=64) for i in range(2)]
         for lo, hi in TOKEN_HALVES:
             project(1, 0, lo, hi, s_copy)
         for e in range(2):
-            project_single(e, 0, T)
+            project_single(e)
         for i in range(2):
             gather(stage[:, SECOND_0 + HALF * i:SECOND_0 + HALF * (i + 1)], 0, 1, HALF * i, HALF * (i + 1))
             weave(0, HALF * i, HALF * (i + 1), stage[:], HALF * i, nc.gpsimd.tensor_copy)
@@ -267,23 +261,33 @@ def tile_moe_prv_lin_bias_kernel(tc, uT, wu, w_words, w_scales, b, gate, offs, p
         for lo, hi in SCALAR_PIECES:
             for e in range(2):
                 gather_single(both_1[lo // HALF][:, HALF + lo % HALF:HALF + lo % HALF + hi - lo], e, lo, hi)
-        weave(1, 0, 256, both_1[0][:], 0, nc.gpsimd.tensor_copy)
-        quantize_x(4, 4, "stage")
-        for e in (2, 3):
+        weave(1, 0, QUARTER, both_1[0][:], 0, nc.gpsimd.tensor_copy)
+        quantize_x([(0, 2), (0, 3), (0, 4), (0, 5)], "stage")
+        expert_pass(2, 0)
+        expert_pass(3, 0)
+        weave(1, QUARTER, HALF, both_1[0][:], QUARTER, v_copy)
+        quantize_x([(1, 0), (1, 1), (0, 0), (0, 1)])
+        for e in (0, 1):
             expert_pass(e, 0)
-        weave(1, 256, 512, both_1[0][:], 256, v_copy)
-        quantize_x(0, 4, "x_codes0")
-        expert(0)
-        expert(1)
-        for lo, hi, first, count, experts in ((512, 768, 8, 4, (2, 3)), (768, 896, 12, 2, (4, 5)), (896, 1024, 14, 1, (6,))):
-            weave(1, lo, hi, both_1[1][:], lo - HALF, v_copy)
-            quantize_x(first, count, f"x_codes{first}")
-            for e in experts:
-                expert(e)
-        quantize_x(15, 1, "x_codes15")
-        expert(7)
+            finish_expert(e)
+        expert_pass(4, 0)
+        expert_pass(5, 0)
+        weave(1, 4 * C, 6 * C, both_1[1][:], 0, v_copy)
+        quantize_x([(0, 6), (0, 7), (1, 2), (1, 3)])
+        finish_expert(2)
+        finish_expert(3)
+        expert_pass(6, 0)
+        expert_pass(7, 0)
+        weave(1, 6 * C, 7 * C, both_1[1][:], 2 * C, v_copy)
+        quantize_x([(1, 4), (1, 5)])
+        finish_expert(4)
+        finish_expert(5)
+        weave(1, 7 * C, 8 * C, both_1[1][:], 3 * C, v_copy)
+        for e in (6, 7):
+            quantize_x([(1, e)])
+            finish_expert(e)
         for e in VECTOR_BIAS:
-            add_bias(e)
+            nc.vector.tensor_scalar_add(y_sb[:, e * C:(e + 1) * C], banks[e][:, 0:C], b_sb[:, e:e + 1])
 
         first = keep.tile([P, T], F32, name="first")
         nc.vector.tensor_tensor(first[:], y_sb[:].indirect(pos1_sb[:]), gate_sb[0][:], MULT)

@@ -187,6 +187,13 @@ def tile_moe_prv_lin_bias_kernel(tc, uT, wu, w_words, w_scales, b, gate, offs, p
                 in_=both.rearrange("p (h n) -> p n h", h=2)[:, column:column + hi - lo, :],
             )
 
+        def weave_lines(a, lo, hi, both, column):
+            at = woven_at(a, lo)
+            v_copy(
+                out=woven[:, at:at + 2 * (hi - lo)].bitcast(F32).rearrange("p (c i h) -> p c h i", h=2, i=4),
+                in_=both.bitcast(F32).rearrange("p (h c i) -> p c h i", h=2, i=4)[:, column // 4:(column + hi - lo) // 4, :, :],
+            )
+
         x_codes = {}
         x_scales = {}
 
@@ -265,24 +272,24 @@ def tile_moe_prv_lin_bias_kernel(tc, uT, wu, w_words, w_scales, b, gate, offs, p
         quantize_x([(0, 2), (0, 3), (0, 4), (0, 5)], "stage")
         expert_pass(2, 0)
         expert_pass(3, 0)
-        weave(1, QUARTER, HALF, both_1[0][:], QUARTER, v_copy)
+        weave_lines(1, QUARTER, HALF, both_1[0][:], QUARTER)
         quantize_x([(1, 0), (1, 1), (0, 0), (0, 1)])
         for e in (0, 1):
             expert_pass(e, 0)
             finish_expert(e)
         expert_pass(4, 0)
         expert_pass(5, 0)
-        weave(1, 4 * C, 6 * C, both_1[1][:], 0, v_copy)
+        weave_lines(1, 4 * C, 6 * C, both_1[1][:], 0)
         quantize_x([(0, 6), (0, 7), (1, 2), (1, 3)])
         finish_expert(2)
         finish_expert(3)
         expert_pass(6, 0)
         expert_pass(7, 0)
-        weave(1, 6 * C, 7 * C, both_1[1][:], 2 * C, v_copy)
+        weave_lines(1, 6 * C, 7 * C, both_1[1][:], 2 * C)
         quantize_x([(1, 4), (1, 5)])
         finish_expert(4)
         finish_expert(5)
-        weave(1, 7 * C, 8 * C, both_1[1][:], 3 * C, v_copy)
+        weave_lines(1, 7 * C, 8 * C, both_1[1][:], 3 * C)
         for e in (6, 7):
             quantize_x([(1, e)])
             finish_expert(e)

@@ -65,10 +65,10 @@ def tile_moe_prv_lin_bias_kernel(tc, uT, wu, w_words, w_scales, b, gate, offs, p
 
         wu_rows = wu.rearrange("(p j) c -> p j c", j=4)
         uT_rows = uT.rearrange("(p j) t -> p j t", j=4)
-        stage = keep.tile([P, STAGE_WORDS], U32, name="stage", tag="stage", align_bytes=64)
-        wu_raw = {key: keep.tile([P, 4, WU_LOAD], F32, name=f"wu_raw{key[0]}{key[1]}", align_bytes=64)[:] for key in ((0, 0), (0, 1), (1, 0))}
+        stage = keep.tile([P, STAGE_WORDS], U32, name="stage", tag="stage", align_bytes=256)
+        wu_raw = {key: keep.tile([P, 4, WU_LOAD], F32, name=f"wu_raw{key[0]}{key[1]}", align_bytes=256)[:] for key in ((0, 0), (0, 1), (1, 0))}
         wu_raw[(1, 1)] = stage[:, LAST_WU:LAST_WU + 4 * WU_LOAD].bitcast(F32).rearrange("p (j c) -> p j c", j=4)
-        u_raw = [keep.tile([P, 4, hi - lo], F32, name=f"u_raw{lo}", tag=f"u_raw{lo}", align_bytes=64) for lo, hi in TOKEN_CHUNKS]
+        u_raw = [keep.tile([P, 4, hi - lo], F32, name=f"u_raw{lo}", tag=f"u_raw{lo}", align_bytes=256) for lo, hi in TOKEN_CHUNKS]
 
         def load_wu(a, c):
             first_column = 512 * a + WU_LOAD * c
@@ -88,7 +88,7 @@ def tile_moe_prv_lin_bias_kernel(tc, uT, wu, w_words, w_scales, b, gate, offs, p
                 in_=scale_rows[r].bitcast(I32),
             )
         per_load = E * PASSES // 2
-        w_codes = [keep.tile([P, per_load, N], I32, name=f"w_codes{i}", align_bytes=64) for i in range(2)]
+        w_codes = [keep.tile([P, per_load, N], I32, name=f"w_codes{i}", align_bytes=256) for i in range(2)]
         word_rows = w_words.rearrange("e a p n r -> p (e a) (n r)")
         for i in range(2):
             nc.sync.dma_start(out=w_codes[i][:], in_=word_rows[:, per_load * i:per_load * (i + 1), :].bitcast(I32))
@@ -119,7 +119,7 @@ def tile_moe_prv_lin_bias_kernel(tc, uT, wu, w_words, w_scales, b, gate, offs, p
             )
 
         def quantize_wu(a, h, tag):
-            wu_codes[(a, h)] = keep.tile([P, 2 * P], U32, name=f"wu_codes{a}{h}", tag=tag, align_bytes=64)
+            wu_codes[(a, h)] = keep.tile([P, 2 * P], U32, name=f"wu_codes{a}{h}", tag=tag, align_bytes=256)
             wu_scales[(a, h)] = keep.tile([P, 2 * P], U8, name=f"wu_scales{a}{h}", align_bytes=64)
             nc.vector.quantize_mx(
                 out=wu_codes[(a, h)][:].bitcast(FP8X4),
@@ -201,7 +201,7 @@ def tile_moe_prv_lin_bias_kernel(tc, uT, wu, w_words, w_scales, b, gate, offs, p
             a0, e0 = parts[0]
             at = woven_at(a0, C * e0)
             name = f"x_codes{a0}{e0}"
-            codes = keep.tile([P, C * len(parts)], U32, name=name, tag=tag or name, align_bytes=64)
+            codes = keep.tile([P, C * len(parts)], U32, name=name, tag=tag or name, align_bytes=256)
             scales = keep.tile([P, C * len(parts)], U8, name=f"x_scales{a0}{e0}", align_bytes=64)
             nc.vector.quantize_mx(
                 out=codes[:].bitcast(FP8X4), scales=scales[:],
@@ -304,6 +304,6 @@ def tile_moe_prv_lin_bias_kernel(tc, uT, wu, w_words, w_scales, b, gate, offs, p
             nc.scalar.activation(second[i][:], y_sb[:].indirect(pos2_sb[:, lo // 16:hi // 16]), COPY)
             nc.vector.tensor_tensor(gated[i][:], second[i][:], gate_sb[1][:, lo:hi], MULT)
         for i, (lo, hi) in enumerate(TOKEN_HALVES):
-            total = keep.tile([P, hi - lo], F32, name=f"total{lo}")
+            total = keep.tile([P, hi - lo], F32, name=f"total{lo}", align_bytes=256)
             nc.vector.tensor_tensor(total[:], first[:, lo:hi], gated[i][:], ADD)
             (nc.sync, nc.scalar)[i].dma_start(out=out[:, lo:hi], in_=total[:])

@@ -210,6 +210,7 @@ def tile_moe_prv_lin_bias_kernel(tc, uT, wu, w_words, w_scales, b, gate, offs, p
             for i, part in enumerate(parts):
                 x_codes[part] = codes[:, C * i:C * (i + 1)]
                 x_scales[part] = scales[:, C * i:C * (i + 1)]
+            return codes[:], scales[:]
 
         y_sb = keep.tile([P, S], F32, name="y_sb")
 
@@ -269,9 +270,16 @@ def tile_moe_prv_lin_bias_kernel(tc, uT, wu, w_words, w_scales, b, gate, offs, p
             for e in range(2):
                 gather_single(both_1[lo // HALF][:, HALF + lo % HALF:HALF + lo % HALF + hi - lo], e, lo, hi)
         weave(1, 0, QUARTER, both_1[0][:], 0, nc.gpsimd.tensor_copy)
-        quantize_x([(0, 2), (0, 3), (0, 4), (0, 5)], "stage")
+        warm_codes, warm_scales = quantize_x([(0, 2), (0, 3), (0, 4), (0, 5)], "stage")
         expert_pass(2, 0)
         expert_pass(3, 0)
+        warm_bank = psum.tile([P, BANK], F32, name="bank")
+        nc.tensor.matmul_mx(
+            out=warm_bank[:],
+            lhsT=w_codes[0][:, 4, :].bitcast(FP8X4), lhsT_scale=w_scale_sb[:, 4 * N:5 * N],
+            rhs=warm_codes.bitcast(FP8X4), rhs_scale=warm_scales,
+            start=True, stop=True,
+        )
         weave_lines(1, QUARTER, HALF, both_1[0][:], QUARTER)
         quantize_x([(1, 0), (1, 1), (0, 0), (0, 1)])
         for e in (0, 1):

@@ -26,12 +26,12 @@ WU_LOAD = 256
 QUADS = WU_LOAD // 4
 HALF = S // 2
 QUARTER = S // 4
-WINDOWS = {(0, 0): 1024, (0, 1): 768, (1, 0): 768}
+WINDOWS = {(0, 0): 1152, (0, 1): 768, (1, 0): 768}
 TOKEN_CHUNKS = ((0, 256), (256, 384), (384, 512))
 TOKEN_HALVES = ((0, 256), (256, 512))
 WU_VECTOR_SHARE = 40
 U_VECTOR_SHARE = 168
-FIRST_CUT = S - QUARTER
+FIRST_CUT = 832
 
 FIRST_0 = 0
 SECOND_0 = FIRST_0 + S
@@ -157,16 +157,16 @@ def tile_moe_prv_lin_bias_kernel(tc, uT, wu, w_words, w_scales, b, gate, offs, p
                 in_=acc.rearrange("p e n -> p n e"),
             )
 
-        def project_single(e):
+        def project_single(e, lo, hi):
             bank = psum.tile([P, BANK], F32, name="bank")
             cols = slice(P * e, P * (e + 1))
             nc.tensor.matmul_mx(
-                out=bank[:],
+                out=bank[:, 0:hi - lo],
                 lhsT=wu_codes[(1, 1)][:, cols].bitcast(FP8X4), lhsT_scale=wu_scales[(1, 1)][:, cols],
-                rhs=u_codes[:].bitcast(FP8X4), rhs_scale=u_scales[:],
+                rhs=u_codes[:, lo:hi].bitcast(FP8X4), rhs_scale=u_scales[:, lo:hi],
                 start=True, stop=True,
             )
-            s_copy(out=singles[:, T * e:T * (e + 1)], in_=bank[:])
+            s_copy(out=singles[:, T * e + lo:T * e + hi], in_=bank[:, 0:hi - lo])
 
         def gather(out, a, h, lo, hi):
             nc.vector.tensor_copy(out, pairs[(a, h)][:].indirect(offs_sb[:, lo // 16:hi // 16]))
@@ -256,10 +256,11 @@ def tile_moe_prv_lin_bias_kernel(tc, uT, wu, w_words, w_scales, b, gate, offs, p
             gather(stage[:, FIRST_0 + lo:FIRST_0 + hi], 0, 0, lo, hi)
             quantize_wu(1, h, f"wu_codes1{h}")
         both_1 = [keep.tile([P, S], U32, name=f"both_1_{i}", align_bytes=64) for i in range(2)]
-        for lo, hi in TOKEN_HALVES:
+        for lo, hi in ((0, 128), (128, 256), (256, 512)):
             project(1, 0, lo, hi, s_copy)
-        for e in range(2):
-            project_single(e)
+        project_single(0, 0, T)
+        for lo, hi in TOKEN_HALVES:
+            project_single(1, lo, hi)
         for i in range(2):
             gather(stage[:, SECOND_0 + HALF * i:SECOND_0 + HALF * (i + 1)], 0, 1, HALF * i, HALF * (i + 1))
             weave(0, HALF * i, HALF * (i + 1), stage[:], HALF * i, nc.gpsimd.tensor_copy)

from contextlib import ExitStack

import concourse.mybir as mybir

F32 = mybir.dt.float32
BF16 = mybir.dt.bfloat16
I32 = mybir.dt.int32
U32 = mybir.dt.uint32
U16 = mybir.dt.uint16
U8 = mybir.dt.uint8
FP8X4 = mybir.dt.float8_e4m3fn_x4
MULT = mybir.AluOpType.mult
ADD = mybir.AluOpType.add
IDENT = mybir.ActivationFunctionType.Identity
COPY = mybir.ActivationFunctionType.Copy

K, T, E, C, N, M = 1024, 512, 8, 128, 128, 512
P = 128
S = E * C
PASSES = K // 512
FLOPS = 2 * M * K * T + 2 * K * N * S

BANKS = 8
BANK = 512
WU_LOAD = 256
QUADS = WU_LOAD // 4
HALF = S // 2
QUARTER = S // 4
WINDOWS = {(0, 0): 1152, (0, 1): 768, (1, 0): 768}
TOKEN_CHUNKS = ((0, 256), (256, 384), (384, 512))
TOKEN_HALVES = ((0, 256), (256, 512))
WU_VECTOR_SHARE = 40
U_VECTOR_SHARE = 168
FIRST_CUT = 832

FIRST_0 = 0
SECOND_0 = FIRST_0 + S
STAGE_WORDS = SECOND_0 + S
LAST_WU = FIRST_0 + FIRST_CUT
WOVEN = ((1, 0), (0, 0), (0, 1), (0, 2), (0, 3), (1, 1), (1, 2), (1, 3))
SCALAR_PIECES = ((0, 256), (256, 512), (512, 768), (768, 896), (896, 1024))
VECTOR_BIAS = (4, 7)


def tile_moe_prv_lin_bias_kernel(tc, uT, wu, w_words, w_scales, b, gate, offs, pos1, pos2, out):
    nc = tc.nc
    with ExitStack() as ctx:
        keep = ctx.enter_context(tc.tile_pool(name="keep", bufs=1))
        psum = ctx.enter_context(tc.psum_pool(name="psum", bufs=BANKS))

        offs_sb = keep.tile([P, S // 16], U16, name="offs_sb")
        pos1_sb = keep.tile([P, T // 16], U16, name="pos1_sb")
        pos2_sb = keep.tile([P, T // 16], U16, name="pos2_sb")

        warm = keep.tile([P, 2], F32, name="warm")
        nc.vector.memset(warm[:, 0:1], 0.0)
        nc.scalar.activation(out=warm[:, 1:2], in_=warm[:, 0:1], func=IDENT)

        w_scale_sb = keep.tile([P, E * PASSES * N], U8, name="w_scale_sb", align_bytes=64)
        nc.vector.memset(w_scale_sb[:].bitcast(I32), 0)
        pairs = {key: keep.tile([P, width], U32, name=f"pairs{key[0]}{key[1]}", align_bytes=64) for key, width in WINDOWS.items()}
        for key, width in WINDOWS.items():
            nc.vector.memset(pairs[key][:, T:width], 0)
        singles = keep.tile([P, 2 * T], BF16, name="singles", align_bytes=64)

        wu_rows = wu.rearrange("(p j) c -> p j c", j=4)
        uT_rows = uT.rearrange("(p j) t -> p j t", j=4)
        stage = keep.tile([P, STAGE_WORDS], U32, name="stage", tag="stage", align_bytes=256)
        wu_raw = {key: keep.tile([P, 4, WU_LOAD], F32, name=f"wu_raw{key[0]}{key[1]}", align_bytes=256)[:] for key in ((0, 0), (0, 1), (1, 0))}
        wu_raw[(1, 1)] = stage[:, LAST_WU:LAST_WU + 4 * WU_LOAD].bitcast(F32).rearrange("p (j c) -> p j c", j=4)
        u_raw = [keep.tile([P, 4, hi - lo], F32, name=f"u_raw{lo}", tag=f"u_raw{lo}", align_bytes=256) for lo, hi in TOKEN_CHUNKS]

        def load_wu(a, c):
            first_column = 512 * a + WU_LOAD * c
            nc.sync.dma_start(out=wu_raw[(a, c)], in_=wu_rows[:, :, first_column:first_column + WU_LOAD])

        load_wu(0, 0)
        load_wu(0, 1)
        for i, (lo, hi) in enumerate(TOKEN_CHUNKS):
            nc.sync.dma_start(out=u_raw[i][:], in_=uT_rows[:, :, lo:hi])
        load_wu(1, 0)
        nc.sync.dma_start(offs_sb[:], offs)
        load_wu(1, 1)
        scale_rows = w_scales.rearrange("e a (q r) n -> r q (e a) n", r=4)
        for r in range(4):
            nc.sync.dma_start(
                out=w_scale_sb[r:P:32, :].bitcast(I32).rearrange("q (g n) -> q g n", n=N // 4),
                in_=scale_rows[r].bitcast(I32),
            )
        per_load = E * PASSES // 2
        w_codes = [keep.tile([P, per_load, N], I32, name=f"w_codes{i}", align_bytes=256) for i in range(2)]
        word_rows = w_words.rearrange("e a p n r -> p (e a) (n r)")
        for i in range(2):
            nc.sync.dma_start(out=w_codes[i][:], in_=word_rows[:, per_load * i:per_load * (i + 1), :].bitcast(I32))
        b_sb = keep.tile([P, E], F32, name="b_sb")
        nc.sync.dma_start(out=b_sb[:], in_=b)
        gate_sb = [keep.tile([P, T], F32, name=f"gate_sb{r}") for r in range(2)]
        for r in range(2):
            nc.sync.dma_start(out=gate_sb[r][:], in_=gate[r])
        nc.sync.dma_start(pos1_sb[:], pos1)
        nc.sync.dma_start(pos2_sb[:], pos2)

        wu_bf = keep.tile([P, 4, P, 4], BF16, name="wu_bf", align_bytes=64)
        wu_codes = {}
        wu_scales = {}
        u_bf = [keep.tile([P, hi - lo, 4], BF16, name=f"u_bf{lo}", align_bytes=64) for lo, hi in TOKEN_CHUNKS]
        u_codes = keep.tile([P, T], U32, name="u_codes", align_bytes=64)
        u_scales = keep.tile([P, T], U8, name="u_scales", align_bytes=64)

        v_copy, s_copy = nc.vector.tensor_copy, nc.scalar.copy

        def g_copy(out, in_):
            nc.gpsimd.tensor_scalar(out.rearrange("p m j t -> p m t j"), in_.rearrange("p m j t -> p m t j"), 1.0, 0.0, MULT, ADD)

        def cast_wu(a, c, copy, lo=0, hi=QUADS):
            copy(
                out=wu_bf[:, :, QUADS * c + lo:QUADS * c + hi, :].rearrange("p t m j -> p m j t"),
                in_=wu_raw[(a, c)][:, :, 4 * lo:4 * hi].rearrange("p j (m t) -> p m j t", t=4),
            )

        def quantize_wu(a, h, tag):
            wu_codes[(a, h)] = keep.tile([P, 2 * P], U32, name=f"wu_codes{a}{h}", tag=tag, align_bytes=256)
            wu_scales[(a, h)] = keep.tile([P, 2 * P], U8, name=f"wu_scales{a}{h}", align_bytes=64)
            nc.vector.quantize_mx(
                out=wu_codes[(a, h)][:].bitcast(FP8X4),
                scales=wu_scales[(a, h)][:],
                in_=wu_bf[:, 2 * h:2 * h + 2, :, :].rearrange("p t m j -> p (t m j)"),
            )

        def cast_u(i, copy, lo=0, hi=128):
            copy(
                out=u_bf[i][:, lo:hi, :].rearrange("p (c n) j -> p c j n", n=4),
                in_=u_raw[i][:, :, lo:hi].rearrange("p j (c n) -> p c j n", n=4),
            )

        def quantize_u(i):
            lo, hi = TOKEN_CHUNKS[i]
            nc.vector.quantize_mx(
                out=u_codes[:, lo:hi].bitcast(FP8X4),
                scales=u_scales[:, lo:hi],
                in_=u_bf[i][:].rearrange("p n j -> p (n j)"),
            )

        def project(a, h, lo, hi, copy):
            bank = psum.tile([P, BANK], F32, name="bank")
            acc = bank[:, 0:2 * (hi - lo)].rearrange("p (e n) -> p e n", e=2)
            for e in range(2):
                cols = slice(P * e, P * (e + 1))
                nc.tensor.matmul_mx(
                    out=acc[:, e, :],
                    lhsT=wu_codes[(a, h)][:, cols].bitcast(FP8X4), lhsT_scale=wu_scales[(a, h)][:, cols],
                    rhs=u_codes[:, lo:hi].bitcast(FP8X4), rhs_scale=u_scales[:, lo:hi],
                    start=True, stop=True,
                )
            copy(
                out=pairs[(a, h)][:, lo:hi].bitcast(BF16).rearrange("p (n e) -> p n e", e=2),
                in_=acc.rearrange("p e n -> p n e"),
            )

        def project_single(e, lo, hi):
            bank = psum.tile([P, BANK], F32, name="bank")
            cols = slice(P * e, P * (e + 1))
            nc.tensor.matmul_mx(
                out=bank[:, 0:hi - lo],
                lhsT=wu_codes[(1, 1)][:, cols].bitcast(FP8X4), lhsT_scale=wu_scales[(1, 1)][:, cols],
                rhs=u_codes[:, lo:hi].bitcast(FP8X4), rhs_scale=u_scales[:, lo:hi],
                start=True, stop=True,
            )
            s_copy(out=singles[:, T * e + lo:T * e + hi], in_=bank[:, 0:hi - lo])

        def gather(out, a, h, lo, hi):
            nc.vector.tensor_copy(out, pairs[(a, h)][:].indirect(offs_sb[:, lo // 16:hi // 16]))

        def gather_single(out, e, lo, hi):
            halves = out.bitcast(BF16).rearrange("p (n e) -> p n e", e=2)
            nc.scalar.activation(halves[:, :, e], singles[:, T * e:T * (e + 1)].indirect(offs_sb[:, lo // 16:hi // 16]), COPY)

        woven = keep.tile([P, 4 * S], U32, name="woven", align_bytes=64)

        def woven_at(a, slot):
            return HALF * WOVEN.index((a, slot // QUARTER)) + 2 * (slot % QUARTER)

        def weave(a, lo, hi, both, column, copy):
            at = woven_at(a, lo)
            copy(
                out=woven[:, at:at + 2 * (hi - lo)].rearrange("p (n h) -> p n h", h=2),
                in_=both.rearrange("p (h n) -> p n h", h=2)[:, column:column + hi - lo, :],
            )

        def weave_lines(a, lo, hi, both, column):
            at = woven_at(a, lo)
            v_copy(
                out=woven[:, at:at + 2 * (hi - lo)].bitcast(F32).rearrange("p (c i h) -> p c h i", h=2, i=4),
                in_=both.bitcast(F32).rearrange("p (h c i) -> p c h i", h=2, i=4)[:, column // 4:(column + hi - lo) // 4, :, :],
            )

        x_codes = {}
        x_scales = {}

        def quantize_x(parts, tag=None):
            a0, e0 = parts[0]
            at = woven_at(a0, C * e0)
            name = f"x_codes{a0}{e0}"
            codes = keep.tile([P, C * len(parts)], U32, name=name, tag=tag or name, align_bytes=256)
            scales = keep.tile([P, C * len(parts)], U8, name=f"x_scales{a0}{e0}", align_bytes=64)
            nc.vector.quantize_mx(
                out=codes[:].bitcast(FP8X4), scales=scales[:],
                in_=woven[:, at:at + 2 * C * len(parts)].bitcast(BF16),
            )
            for i, part in enumerate(parts):
                x_codes[part] = codes[:, C * i:C * (i + 1)]
                x_scales[part] = scales[:, C * i:C * (i + 1)]
            return codes[:], scales[:]

        y_sb = keep.tile([P, S], F32, name="y_sb")

        banks = {}

        def expert_pass(e, a):
            if a == 0:
                banks[e] = psum.tile([P, BANK], F32, name="bank")
            g = e * PASSES + a
            nc.tensor.matmul_mx(
                out=banks[e][:, 0:C],
                lhsT=w_codes[g // per_load][:, g % per_load, :].bitcast(FP8X4), lhsT_scale=w_scale_sb[:, g * N:(g + 1) * N],
                rhs=x_codes[(a, e)].bitcast(FP8X4), rhs_scale=x_scales[(a, e)],
                start=(a == 0), stop=(a == PASSES - 1),
            )

        def finish_expert(e):
            expert_pass(e, 1)
            if e not in VECTOR_BIAS:
                nc.scalar.activation(out=y_sb[:, e * C:(e + 1) * C], in_=banks[e][:, 0:C], func=IDENT, bias=b_sb[:, e:e + 1])

        cast_wu(0, 0, v_copy)
        cast_wu(0, 1, v_copy, 0, WU_VECTOR_SHARE)
        cast_wu(0, 1, s_copy, WU_VECTOR_SHARE, QUADS)
        quantize_wu(0, 0, "wu_codes00")
        cast_u(0, v_copy, 0, U_VECTOR_SHARE)
        cast_u(0, s_copy, U_VECTOR_SHARE, TOKEN_CHUNKS[0][1])
        quantize_u(0)
        cast_u(1, s_copy)
        cast_u(2, v_copy)
        quantize_u(1)
        quantize_u(2)
        quantize_wu(0, 1, f"u_raw{TOKEN_CHUNKS[2][0]}")
        for (lo, hi), copy in zip(TOKEN_CHUNKS, (s_copy, v_copy, s_copy)):
            project(0, 0, lo, hi, copy)
        cast_wu(1, 0, g_copy)
        cast_wu(1, 1, g_copy, 0, QUADS // 2)
        project(0, 1, *TOKEN_HALVES[0], s_copy)
        cast_wu(1, 1, s_copy, QUADS // 2, QUADS)
        project(0, 1, *TOKEN_HALVES[1], s_copy)

        for h, (lo, hi) in enumerate(((0, FIRST_CUT), (FIRST_CUT, S))):
            gather(stage[:, FIRST_0 + lo:FIRST_0 + hi], 0, 0, lo, hi)
            quantize_wu(1, h, f"wu_codes1{h}")
        both_1 = [keep.tile([P, S], U32, name=f"both_1_{i}", align_bytes=64) for i in range(2)]
        for lo, hi in ((0, 128), (128, 256), (256, 512)):
            project(1, 0, lo, hi, s_copy)
        project_single(0, 0, T)
        for lo, hi in TOKEN_HALVES:
            project_single(1, lo, hi)
        for i in range(2):
            gather(stage[:, SECOND_0 + HALF * i:SECOND_0 + HALF * (i + 1)], 0, 1, HALF * i, HALF * (i + 1))
            weave(0, HALF * i, HALF * (i + 1), stage[:], HALF * i, nc.gpsimd.tensor_copy)

        for i in range(2):
            gather(both_1[i][:, 0:HALF], 1, 0, HALF * i, HALF * (i + 1))
        for lo, hi in SCALAR_PIECES:
            for e in range(2):
                gather_single(both_1[lo // HALF][:, HALF + lo % HALF:HALF + lo % HALF + hi - lo], e, lo, hi)
        weave(1, 0, QUARTER, both_1[0][:], 0, nc.gpsimd.tensor_copy)
        warm_codes, warm_scales = quantize_x([(0, 2), (0, 3), (0, 4), (0, 5)], "stage")
        expert_pass(2, 0)
        expert_pass(3, 0)
        warm_bank = psum.tile([P, BANK], F32, name="bank")
        nc.tensor.matmul_mx(
            out=warm_bank[:],
            lhsT=w_codes[0][:, 4, :].bitcast(FP8X4), lhsT_scale=w_scale_sb[:, 4 * N:5 * N],
            rhs=warm_codes.bitcast(FP8X4), rhs_scale=warm_scales,
            start=True, stop=True,
        )
        weave_lines(1, QUARTER, HALF, both_1[0][:], QUARTER)
        quantize_x([(1, 0), (1, 1), (0, 0), (0, 1)])
        for e in (0, 1):
            expert_pass(e, 0)
            finish_expert(e)
        expert_pass(4, 0)
        expert_pass(5, 0)
        weave_lines(1, 4 * C, 6 * C, both_1[1][:], 0)
        quantize_x([(0, 6), (0, 7), (1, 2), (1, 3)])
        finish_expert(2)
        finish_expert(3)
        expert_pass(6, 0)
        expert_pass(7, 0)
        weave_lines(1, 6 * C, 7 * C, both_1[1][:], 2 * C)
        quantize_x([(1, 4), (1, 5)])
        finish_expert(4)
        finish_expert(5)
        weave_lines(1, 7 * C, 8 * C, both_1[1][:], 3 * C)
        for e in (6, 7):
            quantize_x([(1, e)])
            finish_expert(e)
        for e in VECTOR_BIAS:
            nc.vector.tensor_scalar_add(y_sb[:, e * C:(e + 1) * C], banks[e][:, 0:C], b_sb[:, e:e + 1])

        first = keep.tile([P, T], F32, name="first")
        nc.vector.tensor_tensor(first[:], y_sb[:].indirect(pos1_sb[:]), gate_sb[0][:], MULT)
        second = [keep.tile([P, hi - lo], F32, name=f"second{lo}") for lo, hi in TOKEN_HALVES]
        gated = [keep.tile([P, hi - lo], F32, name=f"gated{lo}") for lo, hi in TOKEN_HALVES]
        for i, (lo, hi) in enumerate(TOKEN_HALVES):
            nc.scalar.activation(second[i][:], y_sb[:].indirect(pos2_sb[:, lo // 16:hi // 16]), COPY)
            nc.vector.tensor_tensor(gated[i][:], second[i][:], gate_sb[1][:, lo:hi], MULT)
        for i, (lo, hi) in enumerate(TOKEN_HALVES):
            total = keep.tile([P, hi - lo], F32, name=f"total{lo}", align_bytes=256)
            nc.vector.tensor_tensor(total[:], first[:, lo:hi], gated[i][:], ADD)
            (nc.sync, nc.scalar)[i].dma_start(out=out[:, lo:hi], in_=total[:])
